import numpy as np, ml_dtypes
CORES = [36,164,52,180,100,228,116,244]
N = 8
import mx_ref
BF = ml_dtypes.bfloat16
def gentries(a):
    return np.ascontiguousarray(a.reshape(8, 16, -1).transpose(0, 2, 1)).reshape(8, -1)
def gtable(e):
    e = np.asarray(e); return np.ascontiguousarray(e.reshape(8, -1, 16).transpose(0, 2, 1)).reshape(128, -1).astype(np.int32)
def gcols(t, e):
    v = np.concatenate([t.reshape(8, 16, -1, 4), np.zeros((8, 16, 1, 4), BF)], axis=2)
    return np.ascontiguousarray(np.stack([v[g][:, e[g]] for g in range(8)])).reshape(128, -1)
def tile(rs):
    return np.stack(rs, axis=2).reshape(128, -1).astype(BF)
def pick(q, e):
    c = np.concatenate([q[0].reshape(128, -1, 4), np.zeros((128, 1, 4), np.uint8)], axis=1); s = np.concatenate([q[1], np.ones((16, 1), np.uint8)], axis=1)
    return (np.ascontiguousarray(c[:, e].reshape(128, -1)), np.ascontiguousarray(s[:, e]))
def join(*qs):
    return (np.concatenate([q[0] for q in qs], axis=1), np.concatenate([q[1] for q in qs], axis=1))
def put(q, e, v):
    c, s = q[0].reshape(128, -1, 4).copy(), q[1].copy(); c[:, e] = v[0].reshape(128, -1, 4); s[:, e] = v[1]
    return (c.reshape(128, -1), s)
def pk(c, s):
    return (np.ascontiguousarray(c), mx_ref.live(s))
def emit(q):
    return q[0], q[1]
def packed(v, rng):
    q = [mx_ref.quantize(np.ascontiguousarray(v[r])) for r in range(N)]
    return np.stack([a for a, b in q]), np.stack([mx_ref.plane(b, rng) for a, b in q])
def values_of_codes():
    e, c = np.zeros((128, 128, 4), np.float32), np.zeros((128, 2, 4), np.uint8)
    e[np.arange(128), np.arange(128), 0] = 1
    c[:127, :, 0] = np.arange(256).reshape(2, 128).T[:127]
    return mx_ref.matmul(mx_ref.quantize(e.reshape(128, 512).astype(BF)), (c.reshape(128, 8), np.full((16, 2), 127, np.uint8))).T.reshape(-1).astype(np.float64)
CODE_VALUE, SCALE_VALUE = values_of_codes(), 2.0 ** (np.arange(256) - 127.0)
def decode(q):
    return (CODE_VALUE[q[0]].reshape(16, 8, -1, 4) * SCALE_VALUE[q[1]][:, None, :, None] + 0.0).reshape(128, -1).astype(np.float32)
def f(rng, *shape):
    return mx_ref.flush((rng.standard_normal(shape, dtype=np.float32) * np.exp2(rng.integers(-2, 3, shape[:-1] + (1,)))).astype(BF))
def wide(rng, *shape, cols=0):
    v = rng.standard_normal(shape, dtype=np.float32) * np.exp2(rng.integers(-12, 13, shape)).astype(np.float32)
    if cols: v *= np.repeat(np.exp2(rng.integers(-cols, cols + 1, shape[:-2] + (1, shape[-1] // 4))) * (rng.random(shape[:-2] + (1, shape[-1] // 4)) > 0.0625), 4, axis=-1).astype(np.float32)
    return mx_ref.flush(v.astype(BF))
C = 352
STEP = [4, 1, 2]
def numbers_of(rng):
    return {"x": np.array(f(rng, N, 128, 4 * C)), "u": np.array(f(rng, N, 128, 512)), "v": np.array(f(rng, N, 128, 512))}
def stored(h, t):
    return {"hl": np.stack([gtable(h[r]) for r in range(N)]), "tl": np.stack([gtable(t[r]) for r in range(N)])}
def lists(rng):
    e = np.tile(np.arange(C), (N, 8, 1))
    return stored(rng.permuted(e, axis=2), rng.permuted(e, axis=2))
def layers(rng, still=()):
    w = np.array(f(rng, N, 128, 2048)).reshape(N, 8, 16, 4, 8, 16, 4)
    for i in still:
        w[:, :, i] = 0
        w[:, :, :, :, :, i] = 0
    return w
def weights(rng, w):
    c, s = packed(np.ascontiguousarray(w).reshape(N, 128, 2048), rng)
    return {"wc": c, "ws": s}
def setup_inputs(rng):
    return {**numbers_of(rng), **lists(rng), **weights(rng, layers(rng))}
def setup_inputs_ties(rng):
    d = numbers_of(rng)
    o = rng.permutation(N)
    k = rng.integers(0, 4, (N, 2, 8, C))
    k[o[1]] += 1
    for g in rng.permutation(8)[:4]: k[o[2], :, g] = 1
    x = d["x"].reshape(N, 8, 16, C, 4)
    u = d["u"].reshape(N, 128, 128, 4)
    for i in range(2):
        x[:, :, i] = 0
        x[:, :, i, :, 0] = k[:, i].astype(np.float32).astype(BF)
        u[:, :, i::16] = 0
        for r in range(N):
            for h in range(i, 128, 16): u[r, h, h, 0] = 0.0 if r == o[0] else -1.0 if r == o[1] else 1.0
    a = np.exp2(rng.integers(-3, 4, (8, 1)).astype(np.float32))
    x[:, :, 8:] = 0
    x[:, :, 8, :, 0] = (-1.125 * a).astype(BF)
    x[:, :, 10, :, 0] = (-0.0703125 * a).astype(BF)
    w = layers(rng, [0, 1])
    w[:, :, :, :, :, 8:] = 0
    for g in range(8):
        w[:, g, 8, 0, g, 8, 0] = -28.0
        for b in range(4): w[:, g, 10, b, g, 9, 0] = -2.0 ** (b - 5)
    return {"x": x.reshape(N, 128, 4 * C), "u": u.reshape(N, 128, 512), "v": d["v"], **lists(rng), **weights(rng, w)}
def setup_inputs_near(rng):
    d = numbers_of(rng)
    x = d["x"].astype(np.float32).reshape(N, 8, 16, C, 4)
    x[:, :, 0] = 0
    x[:, :, 8:] = 0
    u = d["u"].reshape(N, 128, 128, 4)
    for i in range(2): u[:, :, i::16] = 0
    w = layers(rng, [0, 8, 9, 10, 11, 12, 13, 14, 15])
    o = rng.permutation(N) % 4
    for r in range(N):
        c = rng.choice([-1.0, 1.0], (8, 1))
        k = 1.0 if o[r] == 0 else 2.0 ** -30
        if o[r] < 2:
            x[r, :, 0, :, 0] = c
            x[r, :, 11, :, 0] = 2.0 ** -10
        x[r, :, 13, :, 0] = rng.integers(0, 2, (8, C)) * (2.0 ** -20 if o[r] < 2 else 2.0 ** -30)
        x[r, :, 15, :, 0] = 2.0 ** -20 if o[r] < 2 else 2.0 ** -29
        for g in range(8):
            w[r, g, 13, 0, g, 12, 0] = 2.0 ** -18 if o[r] < 2 else 2.0 ** -8
            if o[r] < 2: w[r, g, 14, 0, g, 12, 0] = 2.0 ** -6
            w[r, g, 15, 0, g, 15, 0] = 2.0 ** -5 if o[r] < 2 else 16.0
        for i in range(2):
            s = rng.integers(0, 16, (8, C))
            digits = ((s[:, :, None] >> np.arange(4)) & 1) * np.exp2(np.arange(4) - 23.0)
            if o[r] < 2: x[r, :, 8 + i] = digits
            elif o[r] == 2: x[r, :, 8 + i] = digits * rng.choice([-1.0, 1.0], (8, C, 1))
            else:
                x[r, :, 8 + 2 * i, :, 0] = np.where(s < 8, 1.25, 0.0) * 2.0 ** -30 * c
                x[r, :, 9 + 2 * i, :, 0] = np.where(s < 8, 0.0, 1.125) * 2.0 ** -30 * c
                for g in rng.permutation(8)[:4]:
                    e = rng.choice([-1.0, 1.0], C) * 2.0 ** -30
                    x[r, g, 8 + 2 * i, :, 0] = 1.25 * e
                    x[r, g, 9 + 2 * i, :, 0] = -1.125 * e
            for p in range(0, 128, 16):
                u[r, p, p + i, 0] = k if o[r] < 2 else 1.0
                u[r, p + 12, p + i, 0] = k
                if o[r] < 2: u[r, p + 11, p + i, 0] = k
                if o[r] < 3: u[r, p + 8 + i, p + i] = k
                else:
                    u[r, p + 8 + 2 * i, p + i, 0] = k
                    u[r, p + 9 + 2 * i, p + i, 0] = 1.125 * k
        at = [0, C - 1, int(rng.integers(C)), int(rng.integers(C))]
        for g, j in zip(rng.permutation(8)[:4], at): x[r, g, 0, j, 0] = 2.0 ** 29 * rng.choice([-1.0, 1.0])
    return {"x": x.reshape(N, 128, 4 * C).astype(BF), "u": u.reshape(N, 128, 512), "v": d["v"], **lists(rng), **weights(rng, w)}
def setup_inputs_odd(rng):
    d = numbers_of(rng)
    x = (1.0 + (2 * rng.integers(0, 64, (N, 16, 8, C, 4)) + 1) * 2.0 ** -7) * np.exp2(-rng.integers(0, 7, (N, 16, 8, C, 4)).astype(np.float64)) * rng.choice([-1.0, 1.0], (N, 16, 8, C, 4))
    x[:, :, 0, :, 0] = 1.96875 * 2.0 ** 8 * rng.choice([-1.0, 1.0], (N, 16, 1))
    u = d["u"].reshape(N, 128, 128, 4)
    for i in range(2):
        x[:, ::2, 1 + i, :, 0] = (8 + rng.integers(0, 2, (N, 8, C))) * 2.0 ** -8
        u[:, :, i::16] = 0
        for h in range(i, 128, 16): u[:, h + 1, h, 0] = 1.0
    return {"x": x.astype(np.float32).reshape(N, 128, 4 * C).astype(BF), "u": u.reshape(N, 128, 512), "v": d["v"], **lists(rng), **weights(rng, layers(rng, [0, 8]))}
def setup_inputs_ends(rng):
    d = numbers_of(rng)
    x = np.zeros((N, 8, 16, C, 4))
    u = d["u"].astype(np.float32).reshape(N, 128, 128, 4)
    v = d["v"].astype(np.float32)
    w = np.zeros((N, 128, 4, 128, 4), np.float32)
    hh, tt = np.zeros((N, 8, C), np.int64), np.zeros((N, 8, C), np.int64)
    o, e = rng.permutation(N) % 4, rng.permutation(N) % 4
    i, a = np.arange(128), np.arange(C)
    for r in range(N):
        low = -(0.8 + 0.08 * rng.random((8, 16, C, 4))) * 2.0 ** 30
        low[:, 15] = -2.0 ** 30
        tiny = -(1.0 + 0.125 * rng.integers(0, 8, (8, 16, C, 4))) * 2.0 ** -30
        if o[r] == 0: x[r] = low
        if o[r] == 1: x[r] = np.where((rng.random(C) < 0.5)[:, None], -low, low)
        if o[r] == 2: x[r] = tiny
        if o[r] == 3: x[r] = d["x"][r].astype(np.float32).reshape(8, 16, C, 4)[:, :, :1]
        x[r, 0] = tiny[0] * 2.0 ** 20 if o[r] < 2 else tiny[0] if o[r] == 2 else -2.0 ** -30
        for k in range(2):
            h = rng.permutation(8)
            c = np.where(h < 2, 0.0, h % 2 * 2.0 - 1.0)[None, :, None]
            if o[r] < 2: u[r, :, k::16] = c * (0.9 + 0.1 * rng.random((128, 8, 4))) * 2.0 ** 30
            if o[r] == 2: u[r, :, k::16] = c * (1.0 + 0.125 * rng.integers(0, 8, (128, 8, 4))) * 2.0 ** -30
            if o[r] == 3: u[r, :, k::16] *= np.abs(c).astype(np.float32)
        if o[r] < 2: v[r] = rng.choice([-1.0, 1.0], (128, 512)) * (0.9 + 0.1 * rng.random((128, 512))) * 2.0 ** 30
        else: v[r] = rng.choice([-1.0, 1.0], (128, 512)) * (1.0 + 0.125 * rng.integers(0, 8, (128, 512))) * 2.0 ** -30
        k = np.array([0.25, 0.5, 1.0])[rng.permutation(8) % 3] * rng.choice([-1.0, 1.0], 8)
        if o[r] == 2: k[:] = 0.0
        k[0] = 2.0 ** 8 if o[r] > 1 else 2.0 ** -8
        for b in range(4): w[r, i, b, i, b] = np.where((i >= 16) & (i % 16 == 15), 0.0, k[i // 16])
        hh[r] = C - 1 - a if e[r] == 1 else a
        if e[r] == 3: hh[r] = rng.permuted(np.tile(a, (8, 1)), axis=1)
        tt[r] = hh[r] if e[r] < 2 else np.roll(a, 1) if e[r] == 2 else hh[r] ^ 1
    return {"x": x.astype(np.float32).reshape(N, 128, 4 * C).astype(BF), "u": u.reshape(N, 128, 512).astype(BF), "v": v.astype(BF), **stored(hh, tt), **weights(rng, w.astype(BF))}
def setup_inputs_spread(rng):
    d = setup_inputs(rng)
    d["x"] = wide(rng, N, 128, 4 * C, cols=6)
    return d
def check_inputs(d):
    b = []
    for k in ("x", "u", "v"):
        a = np.abs(d[k].astype(np.float32))
        if not (np.isfinite(a).all() and ((a == 0) | (a >= 2.0 ** -30) & (a <= 2.0 ** 30)).all()): b.append("a value of " + k)
    for k in ("hl", "tl"):
        for r in range(N):
            if not (np.sort(gentries(d[k][r]), axis=1) == np.arange(C)).all(): b.append(k + ": every number once in a group")
    none, least, most = [emit(mx_ref.quantize(np.full((128, 16), k, np.float32).astype(BF)))[1][0, 0] for k in (0.0, 2.0 ** -8, 2.0 ** 8)]
    for r in range(N):
        if ((d["wc"][r] == 0x7F) | (d["wc"][r] == 0xFF)).any(): b.append("wc: a code that is no number")
        s = mx_ref.live(d["ws"][r])
        if ((s != none) & ((s < least) | (s > most))).any(): b.append("ws: a scale out of range")
    return b
def ordered(s, a):
    e = np.sort(np.argsort(a, axis=1).reshape(8, -1, 2), axis=2)
    k = np.take_along_axis(s, e.reshape(8, -1), axis=1).reshape(e.shape)
    return np.where((k[:, :, 1] > k[:, :, 0])[:, :, None], e[:, :, ::-1], e).reshape(8, -1)
def transition(s, h, t):
    m = np.zeros((8, C), np.int64)
    np.put_along_axis(m, ordered(s, h), ordered(s, t), axis=1)
    return m
def behind(a, e):
    return np.take_along_axis(a, e, axis=1)
def reference(x, u, v, hl, tl, wc, ws):
    qu = [mx_ref.quantize(u[r]) for r in range(N)]
    lay = [pk(wc[r], ws[r]) for r in range(N)]
    now = [x[r] for r in range(N)]
    head, tail = [gentries(hl[r]) for r in range(N)], [gentries(tl[r]) for r in range(N)]
    for step in STEP:
        way, made = [], []
        for r in range(N):
            s = mx_ref.matmul(qu[r], mx_ref.quantize(now[r])) + np.float32(0.0)
            m0, m1 = transition(s[0::16], head[r], tail[r]), transition(s[1::16], head[r], tail[r])
            way.append(behind(m1, m0))
            z = mx_ref.quantize(((gcols(now[r], m0).astype(np.float32) + gcols(now[r], way[r]).astype(np.float32)) * np.float32(0.5)).astype(BF))
            made.append(mx_ref.quantize(tile([mx_ref.matmul(pick(lay[r], np.arange(128 * b, 128 * b + 128)), z) * np.float32(0.03125) for b in range(4)])))
        for r in range(N):
            p = r ^ step
            far = gcols(decode(made[p]).astype(BF), behind(way[r], way[p]))
            now[r] = (now[r].astype(np.float32) + far.astype(np.float32)).astype(BF)
            head[r], tail[r] = tail[r], behind(head[r], way[p])
    y, tp = np.zeros((N, 128, C), np.float32), np.zeros((N, 8, C), np.float32)
    oc, osc = np.zeros((N, 128, 4 * C), np.uint8), np.zeros((N, 16, C), np.uint8)
    for r in range(N):
        q = mx_ref.quantize(now[r])
        y[r] = mx_ref.matmul(mx_ref.quantize(v[r]), q)
        tp[r] = tail[r]
        oc[r], osc[r] = emit(q)
    return {"y": y, "tp": tp, "oc": oc, "osc": osc}

@@ -1,0 +1,449 @@
+from concourse.mybir import dt, AluOpType, ActivationFunctionType
+
+C = 352
+K = 22
+HV = 176
+SL = 192
+ROUNDS = 3
+STEP = (4, 1, 2)
+HALF = ((0, 160), (160, 352))
+
+SCRATCH = {}
+LOC = {}
+
+
+def _buf(name, cols, dtype, where="sbuf"):
+    SCRATCH[name] = (where, [128, cols], dtype)
+    LOC[name] = (name, 0, cols)
+
+
+def _pack(name, dtype, parts):
+    n = 0
+    for part, cols in parts:
+        LOC[part] = (name, n, cols)
+        n += cols
+    SCRATCH[name] = ("sbuf", [128, n], dtype)
+
+
+for _r in range(ROUNDS + 1):
+    _buf("x%d" % _r, 4 * C, "bfloat16")
+    _buf("xq%d" % _r, C, "float8_e4m3fn_x4")
+    _buf("xp%d" % _r, C, "uint8")
+for _r in range(ROUNDS):
+    _buf("xc%d" % _r, 4 * C, "bfloat16")
+    _buf("hq%d" % _r, C, "float8_e4m3fn_x4")
+    _buf("hp%d" % _r, C, "uint8")
+    _buf("lq%d" % _r, C, "float8_e4m3fn_x4")
+    _buf("lp%d" % _r, C, "uint8")
+    _buf("snd%d" % _r, 2 * K, "uint16")
+    _buf("rcv%d" % _r, 2 * K, "uint16")
+for _n, _c, _t in (("zt", 4 * C, "bfloat16"), ("zq", C, "float8_e4m3fn_x4"), ("zp", C, "uint8"), ("ht", 4 * C, "bfloat16"),
+                   ("vp", 4 * C, "bfloat16"), ("dp", 4 * C, "bfloat16"), ("one", 2048, "bfloat16"), ("eb", 2048, "bfloat16"),
+                   ("eq", 512, "float8_e4m3fn_x4"), ("ep", 512, "uint8"), ("ut", 512, "bfloat16"), ("vt", 512, "bfloat16"),
+                   ("uq", 128, "float8_e4m3fn_x4"), ("up", 128, "uint8"), ("uk", 256, "float8_e4m3fn_x4"), ("ukp", 256, "uint8"),
+                   ("vq", 128, "float8_e4m3fn_x4"), ("vpl", 128, "uint8"), ("wq", 512, "float8_e4m3fn_x4"), ("wpl", 512, "uint8"),
+                   ("hlt", 2 * K, "int32"), ("yt", C, "float32"), ("tpf", C, "float32")):
+    _buf(_n, _c, _t)
+_LISTS = range(ROUNDS + 1)
+_pack("fw", "float32", [("raw%d" % _i, C) for _i in _LISTS] + [("hx%d" % _i, C) for _i in _LISTS] + [("nrm", 3 * SL)] +
+      [(_n, C) for _n in ("s1", "s0", "m1f", "ff", "ga", "lf", "pa", "sc1", "sc2", "sc3", "iof", "tpa")] + [("so1", 2 * SL), ("so0", 2 * SL), ("ab", 2 * C), ("scd", 2 * C), ("wl", 2 * C)] +
+      [("jm", 16), ("wge", 16), ("weq", 16), ("wls", 16), ("wbs", 16), ("icf", 32)] +
+      [("%s%d" % (_n, _r), 24) for _n in ("aw", "bw") for _r in _LISTS] + [("lw", 48), ("hw", 48)] + [(_n, 24) for _n in ("m1w", "m0w", "d1w", "d0w")])
+_pack("bw16", "bfloat16", [(_n, C) for _n in ("g1", "g0", "gn", "bs1", "bs0", "bsn", "wb")] + [("c1", 2 * SL), ("c0", 2 * SL)] + [(_n, HV) for _n in ("xb1", "xb0", "nb")])
+_pack("iw", "int32", [(_n, 4 * K) for _n in ("ew", "half", "less", "vert")] + [(_n, K) for _n in ("w4", "w5", "w6", "w7")] + [("ic", 2 * K), ("ic2", 2 * K)] + [("hs", 2 * K), ("hb", 2 * K), ("hb2", 2 * K), ("uoi", 16)])
+_pack("uw", "uint16", [("eu", 4 * K), ("vu", 4 * K)] + [("pu%d" % _i, K) for _i in _LISTS] +
+      [("nlo", 12 * (ROUNDS + 1)), ("nhi", 12 * (ROUNDS + 1)), ("lu", K), ("ks", 2 * K), ("uo", 16)])
+for _i in range(8):
+    _buf("b%d" % _i, 512, "float32", "psum")
+
+SEMAPHORES = ["qv", "qs", "qt", "qg", "ldh", "ldt", "ldx", "ldu", "ldv", "ldw", "lds", "oy0", "oy1", "otp", "oc", "os0", "os1", "os2", "os3"]
+for _r in range(ROUNDS):
+    for _n in ("rl", "ra", "rb", "rp", "ll", "la", "lb", "lp"):
+        SEMAPHORES.append("%s%d" % (_n, _r))
+
+
+def rank_program(g, core, T, topo):
+    rank = T.rank_of(core)
+    if rank is None:
+        return
+    queue = {"v": g.vector, "s": g.scalar, "t": g.tensor, "g": g, "y": g.sync}
+    seen = {e: {} for e in queue}
+    cnt = {}
+    acc = {}
+
+    def clash(a, b):
+        return a[0] == b[0] and a[1] < b[2] and b[1] < a[2] and (a[3] is None or b[3] is None or a[3] == b[3])
+
+    def emit(eng, fn, reads, writes, sem=None, inc=1, events=None):
+        need = {}
+        for regs, wr in ((reads, False), (writes, True)):
+            for rg in regs:
+                for a in acc.get(rg[0], []):
+                    if not clash(rg, a[0]):
+                        continue
+                    if not wr and not a[1] and not (rg[4] and a[2] != eng):
+                        continue
+                    if seen[eng].get(a[3], 0) < a[4] and need.get(a[3], (0,))[0] < a[4]:
+                        need[a[3]] = (a[4], a[5])
+        for s in list(need):
+            for o in need:
+                if o != s and need[o][1].get(s, 0) >= need[s][0]:
+                    del need[s]
+                    break
+        for s in need:
+            queue[eng].wait_ge(T.sem[s], need[s][0])
+            for o in need[s][1]:
+                seen[eng][o] = max(seen[eng].get(o, 0), need[s][1][o])
+            seen[eng][s] = need[s][0]
+        ins = fn()
+        clock = dict(seen[eng])
+        if events is None:
+            s = sem or "q" + eng
+            cnt[s] = cnt.get(s, 0) + inc
+            ins.then_inc(T.sem[s], inc)
+            ev = (s, cnt[s])
+        else:
+            for s, n in events:
+                cnt[s] = cnt.get(s, 0) + n
+            ev = (events[0][0], cnt[events[0][0]])
+        for regs, wr in ((reads, False), (writes, True)):
+            for rg in regs:
+                old = acc.get(rg[0], [])
+                if wr:
+                    old = [a for a in old if not (rg[1] <= a[0][1] and a[0][2] <= rg[2] and (rg[3] is None or rg[3] == a[0][3]))]
+                old.append((rg, wr, eng, ev[0], ev[1], clock))
+                acc[rg[0]] = old
+
+    def st(name, a=0, b=None, step=1):
+        buf, off, n = LOC[name]
+        a, b = off + a, off + (n if b is None else b)
+        return (T[buf][:, a:b:step] if step > 1 else T[buf][:, a:b], [(buf, a, b, None, False)])
+
+    f = st
+
+    def il(name, a, b, e):
+        return (T[name][:, 4 * a + e:4 * b:4], [(name, 4 * a, 4 * b, e, False)])
+
+    def bank(i, n):
+        return (T["b%d" % i][:, 0:n], [("b%d" % i, 0, 512, None, True)])
+
+    def ind(win, off):
+        return (win[0].indirect(off[0]), win[1] + off[1])
+
+    def u32(v):
+        return (v[0].bitcast(dt.uint32), v[1])
+
+    def tt(out, a, b, op):
+        emit("v", lambda: g.vector.tensor_tensor(out[0], a[0], b[0], op), a[1] + b[1], out[1])
+
+    def ts(out, a, c1, op0, c2=None, op1=None, col=None):
+        if op1 is None:
+            emit("v", lambda: g.vector.tensor_scalar(out[0], a[0], c1, None, op0), a[1] + (col or []), out[1])
+        else:
+            emit("v", lambda: g.vector.tensor_scalar(out[0], a[0], c1, c2, op0, op1), a[1] + (col or []), out[1])
+
+    def cp(out, a):
+        emit("v", lambda: g.vector.tensor_copy(out[0], a[0]), a[1], out[1])
+
+    def fill(out, c):
+        emit("v", lambda: g.vector.memset(out[0], c), [], out[1])
+
+    def act(out, a, scale=None):
+        if scale is None:
+            emit("s", lambda: g.scalar.activation(out[0], a[0], ActivationFunctionType.Copy), a[1], out[1])
+        else:
+            emit("s", lambda: g.scalar.activation(out[0], a[0], ActivationFunctionType.Copy, scale=scale), a[1], out[1])
+
+    def scan(out, a, w):
+        emit("v", lambda: g.vector.tensor_tensor_scan(out[0], a[0], w[0], 0.0, AluOpType.add, AluOpType.mult), a[1] + w[1], out[1])
+
+    def quant(codes, plane, src):
+        emit("v", lambda: g.vector.quantize_mx(codes[0], plane[0], src[0]), src[1], codes[1] + plane[1])
+
+    def mm(out, w, ws, m, ms):
+        emit("t", lambda: g.tensor.matmul_mx(out[0], w[0], ws[0], m[0], ms[0], True, True), w[1] + ws[1] + m[1] + ms[1], out[1])
+
+    def iota(out, pattern, base, cm, imprecise):
+        if imprecise:
+            emit("g", lambda: g.iota(out[0], pattern, base, cm, allow_small_or_imprecise_dtypes=True), [], out[1])
+        else:
+            emit("g", lambda: g.iota(out[0], pattern, base, cm), [], out[1])
+
+    def load(eng, sem, name, src, a=0, b=None, codes=False):
+        o = st(name, a, b)
+        emit(eng, lambda: queue[eng].dma_start(o[0].bitcast(dt.uint8) if codes else o[0], src[:, :]), [], o[1], sem=sem, inc=16)
+
+    def store(eng, sem, dst, src, regs):
+        emit(eng, lambda: queue[eng].dma_start(dst, src), regs, [], sem=sem, inc=16)
+
+    LS, BS = 15, 14
+
+    def wrap(scr, src):
+        scan(f(scr), src, f("wl", 0, C))
+
+    def whole(out, scr):
+        ts(out, st(scr, 15, C, 16), 2.0 ** LS, AluOpType.mult, 0.15, AluOpType.add)
+
+    def bits(out, scr):
+        ts(out, st(scr, 15, C, 16), 2.0 ** (-BS - 1), AluOpType.is_gt)
+
+    add, sub, mult = AluOpType.add, AluOpType.subtract, AluOpType.mult
+
+    load("y", "ldh", "hlt", T.hl, 0, K)
+    load("s", "ldt", "hlt", T.tl, K, 2 * K)
+    load("y", "ldx", "x0", T.x)
+    load("s", "ldu", "ut", T.u)
+    load("y", "ldw", "wq", T.wc, codes=True)
+    load("y", "lds", "wpl", T.ws)
+    load("y", "ldv", "vt", T.v)
+
+    iota(f("ic"), [[0, 2 * K]], 0, 1, False)
+    iota(f("jm"), [[1, 16]], 0, 0, True)
+    iota(f("iof"), [[1, C]], 0, 0, True)
+    iota(f("uoi"), [[1, 2], [16, 8]], 0, 0, False)
+    iota(f("one"), [[0, 2048]], 1, 0, True)
+    ts(f("ic2"), f("ic"), 15, AluOpType.bitwise_and)
+    cp(f("icf", 0, K), f("ic2", 0, K))
+    cp(f("ks"), f("ic2"))
+    own = f("icf", 0, 1)
+    ts(f("wge"), f("jm"), own[0], AluOpType.is_ge, col=own[1])
+    for tab, big, end, out, n in (("wls", 2.0 ** 15, 2.0 ** (-15 - LS), "wl", 2 * K), ("wbs", 2.0 ** 20, 2.0 ** (-20 - BS), "wb", K)):
+        ts(f("weq"), f("jm"), own[0], AluOpType.is_equal, big - 1.0, mult, col=own[1])
+        tt(f(tab), f("weq"), f("wge"), add)
+        ts(f(tab, 15, 16), f(tab, 15, 16), end, mult)
+        act(f(out), ind(f(tab), f("ks", 0, n)))
+    cp(f("uo"), f("uoi"))
+    fill(f("lw"), 0.0)
+    fill(f("hw"), 0.0)
+
+    def side_by_side(r):
+        for b in range(4):
+            o, i = f("xc%d" % r, b * C, b * C + C), il("x%d" % r, 0, C, b)
+            emit("g", lambda: g.affine_select(o[0], i[0], [[0, C]], AluOpType.is_gt, 0.0, 1, 0), i[1], o[1])
+    side_by_side(0)
+    emit("g", lambda: g.affine_select(T.eb[:, :], T.one[:, :], [[1, 4], [-1, 512]], AluOpType.is_equal, 0.0, 0, 4), f("one")[1], f("eb")[1])
+
+    def inverse(i):
+        o, w = ind(f("raw%d" % i), f("eu", K * i, K * i + K)), f("iof")
+        emit("v", lambda: g.vector.tensor_copy(o[0], w[0]), f("eu", K * i, K * i + K)[1] + w[1], f("raw%d" % i)[1])
+
+    def ordered(i, n):
+        rg = ("fw", C * i, C * (i + n))
+        scan(f("scd", 0, n * C), (T.fw[:, rg[1]:rg[2]], [rg + (None, False)]), f("wl", 0, n * C))
+        for out, tmp, op in (("nlo", "lw", AluOpType.min), ("nhi", "hw", AluOpType.max)):
+            for k in range(n):
+                tt(f(tmp, 12 * (i + k), 12 * (i + k) + 11), st("scd", C * k + 15, C * k + HV, 16), st("scd", C * k + HV + 15, C * k + C, 16), op)
+            ts(f(out, 12 * i, 12 * (i + n)), f(tmp, 12 * i, 12 * (i + n)), 2.0 ** LS, AluOpType.mult, 0.15, AluOpType.add)
+
+    def places_a(i):
+        tt(f("nb"), f("raw%d" % i, 0, HV), f("raw%d" % i, HV, C), AluOpType.is_gt)
+
+    def vertices(i, n):
+        a, b = K * i, K * (i + n)
+        ts(f("half", a, b), f("ew", a, b), HV, AluOpType.is_ge)
+        ts(f("less", a, b), f("half", a, b), -HV, mult)
+        tt(f("vert", a, b), f("less", a, b), f("ew", a, b), add)
+        cp(f("vu", a, b), f("vert", a, b))
+
+    def places_b(i):
+        act(f("gn"), ind(f("nb"), f("vu", K * i, K * i + K)))
+
+    def places_c(i):
+        scan(f("bsn"), f("gn"), f("wb"))
+        bits(f("w4"), "bsn")
+        tt(f("w5"), f("w4"), f("half", K * i, K * i + K), AluOpType.not_equal)
+        ts(f("w6"), f("w5"), SL, mult)
+        tt(f("w7"), f("w6"), f("vert", K * i, K * i + K), add)
+        cp(f("pu%d" % i), f("w7"))
+
+    def flat(out, lst):
+        act(out, ind(f("iof"), lst))
+
+    def out_slots(r):
+        for k, n in enumerate(("nlo", "nhi", "nlo")):
+            flat(f("nrm", SL * k, SL * k + SL), f(n, 12 * (r + 1), 12 * (r + 2)))
+
+    def choices_a(r):
+        for k in range(2):
+            act(f("ab", C * k, C * k + C), ind(f("nrm", SL * k, SL * k + 2 * SL), f("pu%d" % r)))
+
+    def choices_b(r):
+        scan(f("scd"), f("ab"), f("wl"))
+        tt(f("bw%d" % r, 0, K), st("scd", C + 15, 2 * C, 16), st("scd", 15, C, 16), sub)
+        ts(f("aw%d" % r, 0, K), st("scd", 15, C, 16), 2.0 ** -BS, mult)
+
+    ts(f("hb"), f("hlt"), 1, AluOpType.bitwise_and)
+    ts(f("hs"), f("hlt"), 1, AluOpType.arith_shift_right)
+    ts(f("hb2"), f("hb"), HV, mult)
+    tt(f("ew", 0, 2 * K), f("hb2"), f("hs"), add)
+    cp(f("eu", 0, 2 * K), f("ew", 0, 2 * K))
+    inverse(0)
+    inverse(1)
+    vertices(0, 2)
+    places_a(0)
+    places_b(0)
+    quant(f("uq"), f("up"), f("ut"))
+    for k in (1, 0):
+        cp(u32(f("uk", 128 * k, 128 * k + 128)), ind(u32(f("uq")), f("uo", 8 * k, 8 * k + 8)))
+        act(f("ukp", 128 * k, 128 * k + 128), ind(f("up"), f("uo", 8 * k, 8 * k + 8)))
+    ordered(0, 2)
+    out_slots(0)
+    places_c(0)
+    choices_a(0)
+    quant(f("xq0"), f("xp0"), f("x0"))
+
+    def far(name, a, b, sem, n):
+        acc.setdefault(name, []).append(((name, a, b, None, False), True, "far", sem, n, {}))
+
+    def send_lists(r):
+        d = T.cores[rank ^ STEP[r]]
+        rid, pid = topo.addr(d, core)
+        n = len(topo.engines(core, d))
+        emit("g", lambda: g.remote_dma(T["rcv%d" % r][:, :], T["snd%d" % r][:, :], T.sem["rl%d" % r], T.sem["ll%d" % r], pid, rid, topo.mask(core, d)),
+             f("snd%d" % r)[1], [], events=[("ll%d" % r, n)])
+        cnt["rl%d" % r] = n
+        far("rcv%d" % r, 0, 2 * K, "rl%d" % r, n)
+
+    def send_run(r, kind, a, b, sem):
+        src, dst = "h%s%d" % (kind, r), "l%s%d" % (kind, r)
+        d = T.cores[rank ^ STEP[r]]
+        rid, pid = topo.addr(d, core)
+        n = len(topo.engines(core, d))
+        rs, ls = "r%s%d" % (sem, r), "l%s%d" % (sem, r)
+        view = (lambda v: v.bitcast(dt.uint8)) if kind == "q" else (lambda v: v)
+        emit("g", lambda: g.remote_dma(view(T[dst][:, a:b]), view(T[src][:, a:b]), T.sem[rs], T.sem[ls], pid, rid, topo.mask(core, d)),
+             f(src, a, b)[1], [], events=[(ls, n)])
+        cnt[rs] = n
+        far(dst, a, b, rs, n)
+
+    for r in range(ROUNDS):
+        X, N, last = "x%d" % r, "x%d" % (r + 1), r == ROUNDS - 1
+        xq, xp, hq, hp, lq, lp, snd, rcv = ["%s%d" % (n, r) for n in ("xq", "xp", "hq", "hp", "lq", "lp", "snd", "rcv")]
+        I, O = r, r + 1
+        if r:
+            quant(f(xq), f(xp), f(X))
+            side_by_side(r)
+        for s in range(2):
+            mm(bank(s, HV), f("uk", 128, 256), f("ukp", 128, 256), f(xq, HV * s, HV * s + HV), f(xp, HV * s, HV * s + HV))
+        mm(bank(2, C), f("uk", 0, 128), f("ukp", 0, 128), f(xq), f(xp))
+        if not last:
+            places_a(O)
+        act(f("s1", 0, HV), bank(0, HV))
+        act(f("s1", HV, C), bank(1, HV))
+        for k in (1, 0):
+            if not k:
+                act(f("s0"), bank(2, C))
+            act(f("so%d" % k), ind(f("s%d" % k), f("nhi", 12 * r, 12 * r + 24)))
+
+        def decide(k):
+            tt(f("c%d" % k), ind(f("s%d" % k), f("nlo", 12 * r, 12 * r + 24)), f("so%d" % k), AluOpType.is_ge)
+            tt(f("xb%d" % k), f("c%d" % k, 0, HV), f("c%d" % k, SL, SL + HV), AluOpType.not_equal)
+            act(f("g%d" % k), ind(f("xb%d" % k), f("vu", K * I, K * I + K)))
+
+        def onward(k):
+            scan(f("bs%d" % k), f("g%d" % k), f("wb"))
+            tt(f("d%dw" % k, 0, K), st("bs%d" % k, 15, C, 16), f("bw%d" % r, 0, K), mult)
+            tt(f("m%dw" % k, 0, K), f("d%dw" % k, 0, K), f("aw%d" % r, 0, K), add)
+            a = K * (1 - k)
+            ts(f(snd, a, a + K), f("m%dw" % k, 0, K), 2.0 ** (LS + BS), mult, 0.1, add)
+
+        def second(b):
+            tt(f("vp", b * C, b * C + C), ind(f("xc%d" % r, b * C, b * C + C), f(snd, 0, K)), il(X, 0, C, b), add)
+        choices_b(r)
+        decide(1)
+        decide(0)
+        if not last:
+            places_b(O)
+        if r < 2:
+            flat(f("hx%d" % r), f("eu", K * r, K * r + K))
+        onward(1)
+        second(0)
+        onward(0)
+        send_lists(r)
+        for b in range(1, 4):
+            second(b)
+
+        def zpart(eng, b, h):
+            a, c = HALF[h]
+            src = ind(f("vp", b * C, b * C + C), f(snd, K + a // 16, K + c // 16))
+            if eng == "s":
+                act(il("zt", a, c, b), src, 0.5)
+            else:
+                ts(il("zt", a, c, b), src, 0.5, mult)
+        for h in range(len(HALF)):
+            for b in range(3):
+                zpart("s", b, h)
+        for h in range(len(HALF)):
+            a, c = HALF[h]
+            zpart("v", 3, h)
+            quant(f("zq", a, c), f("zp", a, c), f("zt", 4 * a, 4 * c))
+            for b in range(4):
+                mm(bank(4 * h + b, c - a), f("wq", 128 * b, 128 * b + 128), f("wpl", 128 * b, 128 * b + 128), f("zq", a, c), f("zp", a, c))
+
+        def hpart(b, h):
+            a, c = HALF[h]
+            if b % 2 == 0 or b == 1 and not last:
+                act(il("ht", a, c, b), bank(4 * h + b, c - a), 0.03125)
+            else:
+                ts(il("ht", a, c, b), bank(4 * h + b, c - a), 0.03125, mult)
+        if not last:
+            places_c(O)
+        for h in range(len(HALF)):
+            a, c = HALF[h]
+            for b in range(4):
+                hpart(b, h)
+            quant(f(hq, a, c), f(hp, a, c), f("ht", 4 * a, 4 * c))
+            send_run(r, "q", a, c, "ab"[h])
+        send_run(r, "p", 0, C, "p")
+        if r == 0:
+            quant(f("eq"), f("ep"), f("eb"))
+        f1, f0 = f(rcv, 0, K), f(rcv, K, 2 * K)
+        act(f("pa"), ind(f("hx%d" % r), f1))
+        act(f("hx%d" % (r + 2)) if r < 2 else f("tpa"), ind(f("pa"), f0))
+        flat(f("m1f"), f(snd, 0, K))
+        act(f("ff"), ind(f("m1f"), f(snd, K, 2 * K)))
+        act(f("ga"), ind(f("ff"), f1))
+        act(f("lf"), ind(f("ga"), f0))
+        if not last:
+            n = r + 2
+            wrap("sc1", f("hx%d" % n))
+            whole(f("eu", K * n, K * n + K), "sc1")
+            inverse(n)
+            ordered(n, 1)
+            if n < ROUNDS:
+                whole(f("ew", K * n, K * n + K), "sc1")
+                vertices(n, 1)
+            out_slots(r + 1)
+            wrap("sc3", f("lf"))
+            whole(f("lu"), "sc3")
+        else:
+            wrap("sc3", f("lf"))
+            whole(f("lu"), "sc3")
+            ts(f("pa"), f("tpa"), HV, AluOpType.is_ge, 2.0 * HV - 1.0, mult)
+            ts(f("ga"), f("tpa"), 2.0, mult)
+            tt(f("tpf"), f("ga"), f("pa"), sub)
+            store("y", "otp", T.tp[:, :], T.tpf[0:128:16, :], f("tpf")[1])
+            quant(f("vq"), f("vpl"), f("vt"))
+        for b in range(4):
+            for h in range(len(HALF)):
+                a, c = HALF[h]
+                mm(bank(4 * h + b, c - a), f("eq", 128 * b, 128 * b + 128), f("ep", 128 * b, 128 * b + 128), f(lq, a, c), f(lp, a, c))
+                (cp if b == 0 and h else act)(f("dp", b * C + a, b * C + c), bank(4 * h + b, c - a))
+        if not last:
+            choices_a(r + 1)
+        for b in range(4):
+            tt(il(N, 0, C, b), ind(f("dp", b * C, b * C + C), f("lu")), il(X, 0, C, b), add)
+    xq, xp = "xq%d" % ROUNDS, "xp%d" % ROUNDS
+    quant(f(xq), f(xp), f("x%d" % ROUNDS))
+    for s in range(2):
+        mm(bank(s, HV), f("vq"), f("vpl"), f(xq, HV * s, HV * s + HV), f(xp, HV * s, HV * s + HV))
+    store("y", "oc", T.oc[:, :], T[xq][:, :].bitcast(dt.uint8), f(xq)[1])
+    for k in range(4):
+        store("y", "os%d" % k, T.osc[4 * k:4 * k + 4, :], T[xp][32 * k:32 * k + 4, :], f(xp)[1])
+    act(f("yt", 0, HV), bank(0, HV))
+    cp(f("yt", HV, C), bank(1, HV))
+    store("s", "oy0", T.y[:, 0:HV], T.yt[:, 0:HV], f("yt", 0, HV)[1])
+    store("y", "oy1", T.y[:, HV:C], T.yt[:, HV:C], f("yt", HV, C)[1])
+    for s in cnt:
+        if seen["y"].get(s, 0) < cnt[s]:
+            g.sync.wait_ge(T.sem[s], cnt[s])

@@ -3,10 +3,25 @@ from concourse.mybir import dt, AluOpType, ActivationFunctionType
 C = 352
 K = 22
 HV = 176
-SL = 192
 ROUNDS = 3
 STEP = (4, 1, 2)
-HALF = ((0, 160), (160, 352))
+RUNS = ((0, 128), (128, 256), (256, 352))
+MEET = ((0, 128), (128, 256), (256, 352))
+LAND = ((0,), (1,), (2,))
+WIDE = 128
+
+
+def wide(run):
+    return (min(run[0], run[1] - WIDE), run[1])
+
+
+def kept(runs, i):
+    return (wide(runs[i])[0] if i else 0, wide(runs[i + 1])[0] if i + 1 < len(runs) else C)
+
+
+SLOT = [0]
+for _run in RUNS:
+    SLOT.append(SLOT[-1] + _run[1] - wide(_run)[0])
 
 SCRATCH = {}
 LOC = {}
@@ -30,36 +45,37 @@ for _r in range(ROUNDS + 1):
     _buf("xq%d" % _r, C, "float8_e4m3fn_x4")
     _buf("xp%d" % _r, C, "uint8")
 for _r in range(ROUNDS):
-    _buf("xc%d" % _r, 4 * C, "bfloat16")
-    _buf("hq%d" % _r, C, "float8_e4m3fn_x4")
-    _buf("hp%d" % _r, C, "uint8")
+    _buf("hq%d" % _r, SLOT[-1], "float8_e4m3fn_x4")
+    _buf("hp%d" % _r, SLOT[-1], "uint8")
     _buf("lq%d" % _r, C, "float8_e4m3fn_x4")
     _buf("lp%d" % _r, C, "uint8")
-    _buf("snd%d" % _r, 2 * K, "uint16")
-    _buf("rcv%d" % _r, 2 * K, "uint16")
-for _n, _c, _t in (("zt", 4 * C, "bfloat16"), ("zq", C, "float8_e4m3fn_x4"), ("zp", C, "uint8"), ("ht", 4 * C, "bfloat16"),
-                   ("vp", 4 * C, "bfloat16"), ("dp", 4 * C, "bfloat16"), ("one", 2048, "bfloat16"), ("eb", 2048, "bfloat16"),
+    _buf("snd%d" % _r, K, "uint16")
+    _buf("rcv%d" % _r, K, "uint16")
+for _n, _c, _t in (("xh", 4 * C, "bfloat16"), ("at", 4 * C, "bfloat16"), ("zt", 4 * C, "bfloat16"), ("zq", SLOT[-1], "float8_e4m3fn_x4"), ("zp", SLOT[-1], "uint8"),
+                   ("ht", 4 * C, "bfloat16"), ("dp", 4 * C, "bfloat16"), ("one", 512, "bfloat16"), ("eb", 2048, "bfloat16"),
                    ("eq", 512, "float8_e4m3fn_x4"), ("ep", 512, "uint8"), ("ut", 512, "bfloat16"), ("vt", 512, "bfloat16"),
                    ("uq", 128, "float8_e4m3fn_x4"), ("up", 128, "uint8"), ("uk", 256, "float8_e4m3fn_x4"), ("ukp", 256, "uint8"),
                    ("vq", 128, "float8_e4m3fn_x4"), ("vpl", 128, "uint8"), ("wq", 512, "float8_e4m3fn_x4"), ("wpl", 512, "uint8"),
-                   ("hlt", 2 * K, "int32"), ("yt", C, "float32"), ("tpf", C, "float32")):
+                   ("hlt", 2 * K, "int32"), ("yt", C, "float32"), ("tpf", C, "float32"), ("ends", 3 * HV, "float16")):
     _buf(_n, _c, _t)
 _LISTS = range(ROUNDS + 1)
-_pack("fw", "float32", [("raw%d" % _i, C) for _i in _LISTS] + [("hx%d" % _i, C) for _i in _LISTS] + [("nrm", 3 * SL)] +
-      [(_n, C) for _n in ("s1", "s0", "m1f", "ff", "ga", "lf", "pa", "sc1", "sc2", "sc3", "iof", "tpa")] + [("so1", 2 * SL), ("so0", 2 * SL), ("ab", 2 * C), ("scd", 2 * C), ("wl", 2 * C)] +
-      [("jm", 16), ("wge", 16), ("weq", 16), ("wls", 16), ("wbs", 16), ("icf", 32)] +
-      [("%s%d" % (_n, _r), 24) for _n in ("aw", "bw") for _r in _LISTS] + [("lw", 48), ("hw", 48)] + [(_n, 24) for _n in ("m1w", "m0w", "d1w", "d0w")])
-_pack("bw16", "bfloat16", [(_n, C) for _n in ("g1", "g0", "gn", "bs1", "bs0", "bsn", "wb")] + [("c1", 2 * SL), ("c0", 2 * SL)] + [(_n, HV) for _n in ("xb1", "xb0", "nb")])
-_pack("iw", "int32", [(_n, 4 * K) for _n in ("ew", "half", "less", "vert")] + [(_n, K) for _n in ("w4", "w5", "w6", "w7")] + [("ic", 2 * K), ("ic2", 2 * K)] + [("hs", 2 * K), ("hb", 2 * K), ("hb2", 2 * K), ("uoi", 16)])
-_pack("uw", "uint16", [("eu", 4 * K), ("vu", 4 * K)] + [("pu%d" % _i, K) for _i in _LISTS] +
-      [("nlo", 12 * (ROUNDS + 1)), ("nhi", 12 * (ROUNDS + 1)), ("lu", K), ("ks", 2 * K), ("uo", 16)])
+_pack("fw", "float32", [("s0", C), ("s1", C)] + [("%s%d" % (_n, _k), HV + 16) for _n in ("hi", "ho") for _k in range(2)] +
+      [(_n, 16) for _n in ("j16", "j4", "ge16", "eq16", "ge4", "eq4", "t16", "t4")] + [(_n, 8) for _n in ("qf", "q4", "q3", "c4", "qh")] +
+      [(_n, 24) for _n in ("e16", "ewc", "bit", "p3")] + [("v3", 3 * K + 6)])
+_pack("bw", "bfloat16", [(_n, C) for _n in ("io", "w16", "w4", "m0f", "m1f", "ff", "lf", "fi", "raw", "he", "hx0", "hx2", "sa", "sb", "sc", "sd")] +
+      [("lh%d" % _i, C) for _i in _LISTS] + [("by%d" % _i, C) for _i in range(2)] + [("%s%d" % (_n, _k), HV) for _n in ("ci", "co") for _k in range(2)] +
+      [("%s%d" % (_n, _k), 3 * HV) for _n in ("sw", "mt") for _k in range(2)])
+_pack("iw", "int32", [(_n, K) for _n in ("ic", "iq", "h2")] + [("vi", 3 * K), ("i4", 2), ("uoi", 16)])
+_pack("uw", "uint16", [("hu", 2 * K), ("vu", 3 * K), ("ks", K), ("uo", 16), ("m16", K)] + [("pu%d" % _i, K) for _i in range(ROUNDS)] +
+      [("nl%d" % _i, K) for _i in _LISTS] + [(_n, 4 * K) for _n in ("m4", "f4", "l4")])
 for _i in range(8):
     _buf("b%d" % _i, 512, "float32", "psum")
 
-SEMAPHORES = ["qv", "qs", "qt", "qg", "ldh", "ldt", "ldx", "ldu", "ldv", "ldw", "lds", "oy0", "oy1", "otp", "oc", "os0", "os1", "os2", "os3"]
+SEMAPHORES = ["qv", "qs", "qt", "qg", "ldh", "ldt", "ldx", "ldu", "ldv", "ldw", "lds", "otp", "os0", "os1", "os2", "os3"]
+SEMAPHORES += ["%s%d" % (_n, _i) for _n in ("oy", "oc") for _i in range(len(MEET))]
 for _r in range(ROUNDS):
-    for _n in ("rl", "ra", "rb", "rp", "ll", "la", "lb", "lp"):
-        SEMAPHORES.append("%s%d" % (_n, _r))
+    for _n in ["l"] + ["q%d" % _i for _i in range(len(RUNS))] + ["p%d" % _i for _i in range(len(LAND))]:
+        SEMAPHORES += ["r%s%d" % (_n, _r), "l%s%d" % (_n, _r)]
 
 
 def rank_program(g, core, T, topo):
@@ -114,18 +130,20 @@ def rank_program(g, core, T, topo):
                 old.append((rg, wr, eng, ev[0], ev[1], clock))
                 acc[rg[0]] = old
 
-    def st(name, a=0, b=None, step=1):
+    def f(name, a=0, b=None, step=1):
         buf, off, n = LOC[name]
         a, b = off + a, off + (n if b is None else b)
         return (T[buf][:, a:b:step] if step > 1 else T[buf][:, a:b], [(buf, a, b, None, False)])
 
-    f = st
+    def third(name, e):
+        buf, off, n = LOC[name]
+        return (T[buf][:, off + e:off + n:3], [(buf, off, off + n, e, False)])
 
     def il(name, a, b, e):
         return (T[name][:, 4 * a + e:4 * b:4], [(name, 4 * a, 4 * b, e, False)])
 
-    def bank(i, n):
-        return (T["b%d" % i][:, 0:n], [("b%d" % i, 0, 512, None, True)])
+    def bank(i, a, b):
+        return (T["b%d" % i][:, a:b], [("b%d" % i, 0, 512, None, True)])
 
     def ind(win, off):
         return (win[0].indirect(off[0]), win[1] + off[1])
@@ -145,17 +163,25 @@ def rank_program(g, core, T, topo):
     def cp(out, a):
         emit("v", lambda: g.vector.tensor_copy(out[0], a[0]), a[1], out[1])
 
-    def fill(out, c):
-        emit("v", lambda: g.vector.memset(out[0], c), [], out[1])
-
     def act(out, a, scale=None):
         if scale is None:
             emit("s", lambda: g.scalar.activation(out[0], a[0], ActivationFunctionType.Copy), a[1], out[1])
         else:
             emit("s", lambda: g.scalar.activation(out[0], a[0], ActivationFunctionType.Copy, scale=scale), a[1], out[1])
 
-    def scan(out, a, w):
-        emit("v", lambda: g.vector.tensor_tensor_scan(out[0], a[0], w[0], 0.0, AluOpType.add, AluOpType.mult), a[1] + w[1], out[1])
+    def affine(out, a, scale, bias, col=None):
+        emit("s", lambda: g.scalar.activation(out[0], a[0], ActivationFunctionType.Identity, bias=bias, scale=scale), a[1] + (col or []), out[1])
+
+    def move(eng, out, a, scale=None):
+        if eng == "s":
+            act(out, a, scale)
+        elif scale is None:
+            cp(out, a)
+        else:
+            ts(out, a, scale, AluOpType.mult)
+
+    def scan(out, a, w, op0=AluOpType.add, op1=AluOpType.mult):
+        emit("v", lambda: g.vector.tensor_tensor_scan(out[0], a[0], w[0], 0.0, op0, op1), a[1] + w[1], out[1])
 
     def quant(codes, plane, src):
         emit("v", lambda: g.vector.quantize_mx(codes[0], plane[0], src[0]), src[1], codes[1] + plane[1])
@@ -163,287 +189,344 @@ def rank_program(g, core, T, topo):
     def mm(out, w, ws, m, ms):
         emit("t", lambda: g.tensor.matmul_mx(out[0], w[0], ws[0], m[0], ms[0], True, True), w[1] + ws[1] + m[1] + ms[1], out[1])
 
-    def iota(out, pattern, base, cm, imprecise):
+    def iota(out, pattern, base, cm, imprecise=True):
         if imprecise:
             emit("g", lambda: g.iota(out[0], pattern, base, cm, allow_small_or_imprecise_dtypes=True), [], out[1])
         else:
             emit("g", lambda: g.iota(out[0], pattern, base, cm), [], out[1])
 
     def load(eng, sem, name, src, a=0, b=None, codes=False):
-        o = st(name, a, b)
+        o = f(name, a, b)
         emit(eng, lambda: queue[eng].dma_start(o[0].bitcast(dt.uint8) if codes else o[0], src[:, :]), [], o[1], sem=sem, inc=16)
 
     def store(eng, sem, dst, src, regs):
         emit(eng, lambda: queue[eng].dma_start(dst, src), regs, [], sem=sem, inc=16)
 
-    LS, BS = 15, 14
-
-    def wrap(scr, src):
-        scan(f(scr), src, f("wl", 0, C))
-
-    def whole(out, scr):
-        ts(out, st(scr, 15, C, 16), 2.0 ** LS, AluOpType.mult, 0.15, AluOpType.add)
-
-    def bits(out, scr):
-        ts(out, st(scr, 15, C, 16), 2.0 ** (-BS - 1), AluOpType.is_gt)
-
     add, sub, mult = AluOpType.add, AluOpType.subtract, AluOpType.mult
+    BIG, LS = 16, 15
+
+    def own(n, scr, flat):
+        scan(f(scr), f(flat), f("w%d" % n))
+
+    def whole16(out, scr):
+        ts(f(out), f(scr, 15, C, 16), 2.0 ** LS, mult, HV + 0.25, add)
+
+    def whole4(out, scr):
+        c4 = f("c4", 0, 1)
+        ts(f(out), f(scr, 3, C, 4), 2.0 ** (LS + 2), mult, c4[0], add, col=c4[1])
 
     load("y", "ldh", "hlt", T.hl, 0, K)
     load("s", "ldt", "hlt", T.tl, K, 2 * K)
+    load("y", "ldu", "ut", T.u)
     load("y", "ldx", "x0", T.x)
-    load("s", "ldu", "ut", T.u)
     load("y", "ldw", "wq", T.wc, codes=True)
     load("y", "lds", "wpl", T.ws)
     load("y", "ldv", "vt", T.v)
 
-    iota(f("ic"), [[0, 2 * K]], 0, 1, False)
-    iota(f("jm"), [[1, 16]], 0, 0, True)
-    iota(f("iof"), [[1, C]], 0, 0, True)
+    iota(f("ic"), [[0, K]], 0, 1, False)
+    iota(f("j16"), [[1, 16]], 0, 0)
+    iota(f("j4"), [[0, 4], [1, 4]], 0, 0)
+    iota(f("io"), [[1, C]], -HV, 0)
     iota(f("uoi"), [[1, 2], [16, 8]], 0, 0, False)
-    iota(f("one"), [[0, 2048]], 1, 0, True)
-    ts(f("ic2"), f("ic"), 15, AluOpType.bitwise_and)
-    cp(f("icf", 0, K), f("ic2", 0, K))
-    cp(f("ks"), f("ic2"))
-    own = f("icf", 0, 1)
-    ts(f("wge"), f("jm"), own[0], AluOpType.is_ge, col=own[1])
-    for tab, big, end, out, n in (("wls", 2.0 ** 15, 2.0 ** (-15 - LS), "wl", 2 * K), ("wbs", 2.0 ** 20, 2.0 ** (-20 - BS), "wb", K)):
-        ts(f("weq"), f("jm"), own[0], AluOpType.is_equal, big - 1.0, mult, col=own[1])
-        tt(f(tab), f("weq"), f("wge"), add)
-        ts(f(tab, 15, 16), f(tab, 15, 16), end, mult)
-        act(f(out), ind(f(tab), f("ks", 0, n)))
-    cp(f("uo"), f("uoi"))
-    fill(f("lw"), 0.0)
-    fill(f("hw"), 0.0)
+    iota(f("e16", 0, K), [[16, K]], -HV, 0)
+    for k in range(2):
+        iota(third("sw%d" % k, 0), [[0, HV]], 0, 0)
+        iota(third("sw%d" % k, 2), [[0, HV]], -1, 0)
+    iota(f("one"), [[0, 512]], 1, 0)
+    for b in range(4):
+        o = f("eb", 512 * b, 512 * b + 512)
+        emit("g", lambda: g.affine_select(o[0], T.one[:, :], [[-1, 512]], AluOpType.is_equal, 0.0, b, 4), f("one")[1], o[1])
+    ts(f("iq"), f("ic"), 15, AluOpType.bitwise_and)
+    cp(f("qf", 0, 2), f("iq", 0, 2))
+    ts(f("i4"), f("iq", 0, 2), 2, AluOpType.arith_shift_right)
+    cp(f("ks"), f("iq"))
+    cp(f("q4", 0, 2), f("i4"))
+    qf, q4 = f("qf", 0, 1), f("q4", 0, 1)
+    tabs = ((16, qf), (4, q4))
+    for n, at in tabs:
+        ts(f("ge%d" % n), f("j%d" % n), at[0], AluOpType.is_ge, col=at[1])
+        ts(f("eq%d" % n), f("j%d" % n), at[0], AluOpType.is_equal, 2.0 ** BIG - 1.0, mult, col=at[1])
+    for n, at in tabs:
+        tt(f("t%d" % n), f("eq%d" % n), f("ge%d" % n), add)
+    for n, at in tabs:
+        ts(f("t%d" % n, n - 1, 16, n), f("t%d" % n, n - 1, 16, n), 2.0 ** (-BIG - LS), mult)
+    affine(f("q3", 0, 1), q4, -4.0, qf[0], qf[1])
+    affine(f("qh", 0, 1), qf, 2.0 ** -LS, 2.0 ** (-LS - 1))
+    affine(f("c4", 0, 1), f("q3", 0, 1), 1.0, 4 * HV + 0.25)
+    for n, at in tabs:
+        act(f("w%d" % n), ind(f("t%d" % n), f("ks")))
+    affine(f("ewc", 0, K), f("e16", 0, K), 2.0 ** -LS, f("qh", 0, 1)[0], f("qh", 0, 1)[1])
 
-    def side_by_side(r):
-        for b in range(4):
-            o, i = f("xc%d" % r, b * C, b * C + C), il("x%d" % r, 0, C, b)
-            emit("g", lambda: g.affine_select(o[0], i[0], [[0, C]], AluOpType.is_gt, 0.0, 1, 0), i[1], o[1])
-    side_by_side(0)
-    emit("g", lambda: g.affine_select(T.eb[:, :], T.one[:, :], [[1, 4], [-1, 512]], AluOpType.is_equal, 0.0, 0, 4), f("one")[1], f("eb")[1])
+    def lo(i):
+        return f("nl%d" % i, 0, K // 2)
 
-    def inverse(i):
-        o, w = ind(f("raw%d" % i), f("eu", K * i, K * i + K)), f("iof")
-        emit("v", lambda: g.vector.tensor_copy(o[0], w[0]), f("eu", K * i, K * i + K)[1] + w[1], f("raw%d" % i)[1])
+    def hi(i):
+        return f("nl%d" % i, K // 2 - 1, K)
 
-    def ordered(i, n):
-        rg = ("fw", C * i, C * (i + n))
-        scan(f("scd", 0, n * C), (T.fw[:, rg[1]:rg[2]], [rg + (None, False)]), f("wl", 0, n * C))
-        for out, tmp, op in (("nlo", "lw", AluOpType.min), ("nhi", "hw", AluOpType.max)):
-            for k in range(n):
-                tt(f(tmp, 12 * (i + k), 12 * (i + k) + 11), st("scd", C * k + 15, C * k + HV, 16), st("scd", C * k + HV + 15, C * k + C, 16), op)
-            ts(f(out, 12 * i, 12 * (i + n)), f(tmp, 12 * i, 12 * (i + n)), 2.0 ** LS, AluOpType.mult, 0.15, AluOpType.add)
+    def scatter(win, lst):
+        o = ind(win, lst)
+        emit("v", lambda: g.vector.tensor_copy(o[0], f("io")[0]), lst[1] + f("io")[1], win[1])
 
-    def places_a(i):
-        tt(f("nb"), f("raw%d" % i, 0, HV), f("raw%d" % i, HV, C), AluOpType.is_gt)
+    def sort_slots(i, a, b):
+        tt(f("lh%d" % i, 0, HV), a, b, AluOpType.min)
+        tt(f("lh%d" % i, HV, C), a, b, AluOpType.max)
 
-    def vertices(i, n):
+    def vertices(step, i, n, src):
         a, b = K * i, K * (i + n)
-        ts(f("half", a, b), f("ew", a, b), HV, AluOpType.is_ge)
-        ts(f("less", a, b), f("half", a, b), -HV, mult)
-        tt(f("vert", a, b), f("less", a, b), f("ew", a, b), add)
-        cp(f("vu", a, b), f("vert", a, b))
+        if step == 0:
+            ts(f("vi", a, b), src, 1, AluOpType.arith_shift_right)
+        else:
+            cp(f("vu", a, b), f("vi", a, b))
+            ts(f("v3", a, b), f("vi", a, b), 3, mult, 1, add)
 
-    def places_b(i):
-        act(f("gn"), ind(f("nb"), f("vu", K * i, K * i + K)))
+    def places(step, i):
+        if step == 0:
+            act(f("he"), ind(f("lh%d" % i, HV, C), f("vu", K * i, K * i + K)))
+        elif step == 1:
+            own(16, "sb", "he")
+        elif step == 2:
+            tt(f("bit", 0, K), f("sb", 15, C, 16), f("ewc", 0, K), AluOpType.is_lt)
+        elif step == 3:
+            tt(f("p3", 0, K), f("bit", 0, K), f("v3", K * i, K * i + K), add)
+        else:
+            cp(f("pu%d" % i), f("p3", 0, K))
 
-    def places_c(i):
-        scan(f("bsn"), f("gn"), f("wb"))
-        bits(f("w4"), "bsn")
-        tt(f("w5"), f("w4"), f("half", K * i, K * i + K), AluOpType.not_equal)
-        ts(f("w6"), f("w5"), SL, mult)
-        tt(f("w7"), f("w6"), f("vert", K * i, K * i + K), add)
-        cp(f("pu%d" % i), f("w7"))
+    def out_edges(step, r):
+        a, b = f("lh%d" % (r + 1), 0, HV), f("lh%d" % (r + 1), HV, C)
+        if step == 0:
+            tt(third("ends", 0), b, a, sub)
+        elif step == 1:
+            cp(third("ends", 1), a)
+        else:
+            tt(third("ends", 2), b, a, add)
 
-    def flat(out, lst):
-        act(out, ind(f("iof"), lst))
+    def codes_x(r, run):
+        a, b = wide(run)
+        quant(f("xq%d" % r, a, b), f("xp%d" % r, a, b), f("x%d" % r, 4 * a, 4 * b))
 
-    def out_slots(r):
-        for k, n in enumerate(("nlo", "nhi", "nlo")):
-            flat(f("nrm", SL * k, SL * k + SL), f(n, 12 * (r + 1), 12 * (r + 2)))
-
-    def choices_a(r):
+    def scores(r, run, i):
+        a, b = wide(run)
         for k in range(2):
-            act(f("ab", C * k, C * k + C), ind(f("nrm", SL * k, SL * k + 2 * SL), f("pu%d" % r)))
+            mm(bank(2 * i + k, 0, b - a), f("uk", 128 * k, 128 * k + 128), f("ukp", 128 * k, 128 * k + 128), f("xq%d" % r, a, b), f("xp%d" % r, a, b))
 
-    def choices_b(r):
-        scan(f("scd"), f("ab"), f("wl"))
-        tt(f("bw%d" % r, 0, K), st("scd", C + 15, 2 * C, 16), st("scd", 15, C, 16), sub)
-        ts(f("aw%d" % r, 0, K), st("scd", 15, C, 16), 2.0 ** -BS, mult)
+    def keep_score(eng, run, i, k):
+        a = wide(run)[0]
+        move(eng, f("s%d" % k, run[0], run[1]), bank(2 * i + k, run[0] - a, run[1] - a))
 
-    ts(f("hb"), f("hlt"), 1, AluOpType.bitwise_and)
-    ts(f("hs"), f("hlt"), 1, AluOpType.arith_shift_right)
-    ts(f("hb2"), f("hb"), HV, mult)
-    tt(f("ew", 0, 2 * K), f("hb2"), f("hs"), add)
-    cp(f("eu", 0, 2 * K), f("ew", 0, 2 * K))
-    inverse(0)
-    inverse(1)
-    vertices(0, 2)
-    places_a(0)
-    places_b(0)
+    def halve(eng, r, run):
+        move(eng, f("xh", 4 * run[0], 4 * run[1]), f("x%d" % r, 4 * run[0], 4 * run[1]), 0.5)
+
+    def second(k, side, i):
+        act(f("h%s%d" % (side, k)), ind(f("s%d" % k), hi(i)))
+
+    def higher(k, side, i):
+        tt(f("c%s%d" % (side, k)), ind(f("s%d" % k), lo(i)), f("h%s%d" % (side, k), 16), AluOpType.is_ge)
+
+    def crossed(k):
+        tt(third("sw%d" % k, 1), f("ci%d" % k), f("co%d" % k), AluOpType.not_equal)
+
+    def table(k):
+        scan(f("mt%d" % k), f("sw%d" % k), f("ends"), mult, add)
+
+    cp(f("hu"), f("hlt"))
+    vertices(0, 0, 2, f("hlt"))
+    scatter(f("by0"), f("hu", 0, K))
+    act(f("hx0"), ind(f("io"), f("hu", 0, K)))
+    vertices(1, 0, 2, None)
+    sort_slots(0, f("by0", 0, C, 2), f("by0", 1, C, 2))
     quant(f("uq"), f("up"), f("ut"))
-    for k in (1, 0):
-        cp(u32(f("uk", 128 * k, 128 * k + 128)), ind(u32(f("uq")), f("uo", 8 * k, 8 * k + 8)))
-        act(f("ukp", 128 * k, 128 * k + 128), ind(f("up"), f("uo", 8 * k, 8 * k + 8)))
-    ordered(0, 2)
-    out_slots(0)
-    places_c(0)
-    choices_a(0)
-    quant(f("xq0"), f("xp0"), f("x0"))
+    cp(f("uo"), f("uoi"))
+    own(16, "sa", "lh0")
+    cp(u32(f("uk")), ind(u32(f("uq")), f("uo")))
+    act(f("ukp"), ind(f("up"), f("uo")))
+    places(0, 0)
+    halve("s", 0, RUNS[0])
+    whole16("nl0", "sa")
+    codes_x(0, (0, C))
+    scores(0, (0, C), 0)
+    scatter(f("by1"), f("hu", K, 2 * K))
+    for k in range(2):
+        keep_score("s", (0, C), 0, k)
+        second(k, "i", 0)
+    places(1, 0)
+    sort_slots(1, f("by1", 0, C, 2), f("by1", 1, C, 2))
+    places(2, 0)
+    own(16, "sa", "lh1")
+    places(3, 0)
+    whole16("nl1", "sa")
+    places(4, 0)
 
-    def far(name, a, b, sem, n):
-        acc.setdefault(name, []).append(((name, a, b, None, False), True, "far", sem, n, {}))
-
-    def send_lists(r):
-        d = T.cores[rank ^ STEP[r]]
-        rid, pid = topo.addr(d, core)
-        n = len(topo.engines(core, d))
-        emit("g", lambda: g.remote_dma(T["rcv%d" % r][:, :], T["snd%d" % r][:, :], T.sem["rl%d" % r], T.sem["ll%d" % r], pid, rid, topo.mask(core, d)),
-             f("snd%d" % r)[1], [], events=[("ll%d" % r, n)])
-        cnt["rl%d" % r] = n
-        far("rcv%d" % r, 0, 2 * K, "rl%d" % r, n)
-
-    def send_run(r, kind, a, b, sem):
-        src, dst = "h%s%d" % (kind, r), "l%s%d" % (kind, r)
-        d = T.cores[rank ^ STEP[r]]
-        rid, pid = topo.addr(d, core)
-        n = len(topo.engines(core, d))
+    def send(r, src, a, dst, c, d, sem, codes=False):
+        to = T.cores[rank ^ STEP[r]]
+        rid, pid = topo.addr(to, core)
+        n = len(topo.engines(core, to))
         rs, ls = "r%s%d" % (sem, r), "l%s%d" % (sem, r)
-        view = (lambda v: v.bitcast(dt.uint8)) if kind == "q" else (lambda v: v)
-        emit("g", lambda: g.remote_dma(view(T[dst][:, a:b]), view(T[src][:, a:b]), T.sem[rs], T.sem[ls], pid, rid, topo.mask(core, d)),
-             f(src, a, b)[1], [], events=[(ls, n)])
+        view = (lambda v: v.bitcast(dt.uint8)) if codes else (lambda v: v)
+        emit("g", lambda: g.remote_dma(view(T[dst][:, c:d]), view(T[src][:, a:a + d - c]), T.sem[rs], T.sem[ls], pid, rid, topo.mask(core, to)),
+             f(src, a, a + d - c)[1], [], events=[(ls, n)])
         cnt[rs] = n
-        far(dst, a, b, rs, n)
+        acc.setdefault(dst, []).append(((dst, c, d, None, False), True, "far", rs, n, {}))
 
     for r in range(ROUNDS):
         X, N, last = "x%d" % r, "x%d" % (r + 1), r == ROUNDS - 1
-        xq, xp, hq, hp, lq, lp, snd, rcv = ["%s%d" % (n, r) for n in ("xq", "xp", "hq", "hp", "lq", "lp", "snd", "rcv")]
-        I, O = r, r + 1
-        if r:
-            quant(f(xq), f(xp), f(X))
-            side_by_side(r)
-        for s in range(2):
-            mm(bank(s, HV), f("uk", 128, 256), f("ukp", 128, 256), f(xq, HV * s, HV * s + HV), f(xp, HV * s, HV * s + HV))
-        mm(bank(2, C), f("uk", 0, 128), f("ukp", 0, 128), f(xq), f(xp))
-        if not last:
-            places_a(O)
-        act(f("s1", 0, HV), bank(0, HV))
-        act(f("s1", HV, C), bank(1, HV))
-        for k in (1, 0):
-            if not k:
-                act(f("s0"), bank(2, C))
-            act(f("so%d" % k), ind(f("s%d" % k), f("nhi", 12 * r, 12 * r + 24)))
-
-        def decide(k):
-            tt(f("c%d" % k), ind(f("s%d" % k), f("nlo", 12 * r, 12 * r + 24)), f("so%d" % k), AluOpType.is_ge)
-            tt(f("xb%d" % k), f("c%d" % k, 0, HV), f("c%d" % k, SL, SL + HV), AluOpType.not_equal)
-            act(f("g%d" % k), ind(f("xb%d" % k), f("vu", K * I, K * I + K)))
+        hq, hp, lq, lp, snd, rcv = ["%s%d" % (n, r) for n in ("hq", "hp", "lq", "lp", "snd", "rcv")]
 
         def onward(k):
-            scan(f("bs%d" % k), f("g%d" % k), f("wb"))
-            tt(f("d%dw" % k, 0, K), st("bs%d" % k, 15, C, 16), f("bw%d" % r, 0, K), mult)
-            tt(f("m%dw" % k, 0, K), f("d%dw" % k, 0, K), f("aw%d" % r, 0, K), add)
-            a = K * (1 - k)
-            ts(f(snd, a, a + K), f("m%dw" % k, 0, K), 2.0 ** (LS + BS), mult, 0.1, add)
+            act(f("m%df" % k), ind(f("mt%d" % k), f("pu%d" % r)))
 
-        def second(b):
-            tt(f("vp", b * C, b * C + C), ind(f("xc%d" % r, b * C, b * C + C), f(snd, 0, K)), il(X, 0, C, b), add)
-        choices_b(r)
-        decide(1)
-        decide(0)
-        if not last:
-            places_b(O)
-        if r < 2:
-            flat(f("hx%d" % r), f("eu", K * r, K * r + K))
-        onward(1)
-        second(0)
-        onward(0)
-        send_lists(r)
-        for b in range(1, 4):
-            second(b)
-
-        def zpart(eng, b, h):
-            a, c = HALF[h]
-            src = ind(f("vp", b * C, b * C + C), f(snd, K + a // 16, K + c // 16))
-            if eng == "s":
-                act(il("zt", a, c, b), src, 0.5)
-            else:
-                ts(il("zt", a, c, b), src, 0.5, mult)
-        for h in range(len(HALF)):
-            for b in range(3):
-                zpart("s", b, h)
-        for h in range(len(HALF)):
-            a, c = HALF[h]
-            zpart("v", 3, h)
-            quant(f("zq", a, c), f("zp", a, c), f("zt", 4 * a, 4 * c))
-            for b in range(4):
-                mm(bank(4 * h + b, c - a), f("wq", 128 * b, 128 * b + 128), f("wpl", 128 * b, 128 * b + 128), f("zq", a, c), f("zp", a, c))
-
-        def hpart(b, h):
-            a, c = HALF[h]
-            if b % 2 == 0 or b == 1 and not last:
-                act(il("ht", a, c, b), bank(4 * h + b, c - a), 0.03125)
-            else:
-                ts(il("ht", a, c, b), bank(4 * h + b, c - a), 0.03125, mult)
-        if not last:
-            places_c(O)
-        for h in range(len(HALF)):
-            a, c = HALF[h]
-            for b in range(4):
-                hpart(b, h)
-            quant(f(hq, a, c), f(hp, a, c), f("ht", 4 * a, 4 * c))
-            send_run(r, "q", a, c, "ab"[h])
-        send_run(r, "p", 0, C, "p")
         if r == 0:
-            quant(f("eq"), f("ep"), f("eb"))
-        f1, f0 = f(rcv, 0, K), f(rcv, K, 2 * K)
-        act(f("pa"), ind(f("hx%d" % r), f1))
-        act(f("hx%d" % (r + 2)) if r < 2 else f("tpa"), ind(f("pa"), f0))
-        flat(f("m1f"), f(snd, 0, K))
-        act(f("ff"), ind(f("m1f"), f(snd, K, 2 * K)))
-        act(f("ga"), ind(f("ff"), f1))
-        act(f("lf"), ind(f("ga"), f0))
-        if not last:
-            n = r + 2
-            wrap("sc1", f("hx%d" % n))
-            whole(f("eu", K * n, K * n + K), "sc1")
-            inverse(n)
-            ordered(n, 1)
-            if n < ROUNDS:
-                whole(f("ew", K * n, K * n + K), "sc1")
-                vertices(n, 1)
-            out_slots(r + 1)
-            wrap("sc3", f("lf"))
-            whole(f("lu"), "sc3")
+            for k in range(2):
+                second(k, "o", 1)
+            halve("s", 0, (RUNS[0][1], C))
+            higher(0, "i", r)
+            for step in range(3):
+                out_edges(step, r)
+            higher(0, "o", r + 1)
         else:
-            wrap("sc3", f("lf"))
-            whole(f("lu"), "sc3")
-            ts(f("pa"), f("tpa"), HV, AluOpType.is_ge, 2.0 * HV - 1.0, mult)
-            ts(f("ga"), f("tpa"), 2.0, mult)
-            tt(f("tpf"), f("ga"), f("pa"), sub)
-            store("y", "otp", T.tp[:, :], T.tpf[0:128:16, :], f("tpf")[1])
-            quant(f("vq"), f("vpl"), f("vt"))
-        for b in range(4):
-            for h in range(len(HALF)):
-                a, c = HALF[h]
-                mm(bank(4 * h + b, c - a), f("eq", 128 * b, 128 * b + 128), f("ep", 128 * b, 128 * b + 128), f(lq, a, c), f(lp, a, c))
-                (cp if b == 0 and h else act)(f("dp", b * C + a, b * C + c), bank(4 * h + b, c - a))
+            for k in range(2):
+                second(k, "i", r)
+                second(k, "o", r + 1)
+            higher(0, "i", r)
+            higher(0, "o", r + 1)
+        higher(1, "i", r)
+        crossed(0)
+        table(0)
+        onward(0)
+        higher(1, "o", r + 1)
+        crossed(1)
+        table(1)
+        onward(1)
+        own(4, "sc", "m0f")
+        own(16, "sd", "m0f")
+        whole4("m4", "sc")
+        whole16("m16", "sd")
+        if r == 0:
+            quant(f("eq", 0, 256), f("ep", 0, 256), f("eb", 0, 1024))
+        if r == 1:
+            own(16, "sb", "hx2")
+            whole16("h2", "sb")
+
+        def first(i):
+            a, b = RUNS[i]
+            act(f("at", 4 * a, 4 * b), ind(f(X), f("m4", a // 4, b // 4)), 0.5)
+
+        def both(i):
+            a, b = RUNS[i]
+            tt(f("zt", 4 * a, 4 * b), ind(f("xh"), f("f4", a // 4, b // 4)), f("at", 4 * a, 4 * b), add)
+
+        def layer(i):
+            a, b = wide(RUNS[i])
+            zq, zp = f("zq", SLOT[i], SLOT[i + 1]), f("zp", SLOT[i], SLOT[i + 1])
+            quant(zq, zp, f("zt", 4 * a, 4 * b))
+            for e in range(4):
+                mm(bank(4 * (i % 2) + e, 0, b - a), f("wq", 128 * e, 128 * e + 128), f("wpl", 128 * e, 128 * e + 128), zq, zp)
+
+        def made(i, engs):
+            a, b = RUNS[i]
+            o = wide(RUNS[i])[0]
+            for e in range(4):
+                move(engs[e], il("ht", a, b, e), bank(4 * (i % 2) + e, a - o, b - o), 0.03125)
+
+        def away(i):
+            a, b = wide(RUNS[i])
+            quant(f(hq, SLOT[i], SLOT[i + 1]), f(hp, SLOT[i], SLOT[i + 1]), f("ht", 4 * a, 4 * b))
+            send(r, hq, SLOT[i] + RUNS[i][0] - a, lq, RUNS[i][0], b, "q%d" % i, True)
+            for n, runs in enumerate(LAND):
+                if runs[-1] == i:
+                    j = runs[0]
+                    send(r, hp, SLOT[j] + RUNS[j][0] - wide(RUNS[j])[0], lp, RUNS[j][0], b, "p%d" % n)
+
+        first(0)
+        cp(f("ff"), ind(f("m1f"), f("m16")))
+        own(4, "sc", "ff")
+        own(16, "sd", "ff")
+        whole4("f4", "sc")
+        whole16(snd, "sd")
+        send(r, snd, 0, rcv, 0, K, "l")
+        first(1)
+        both(0)
+        layer(0)
+        first(2)
+        made(0, "ssss")
+        both(1)
+        if r == 1:
+            vertices(0, 2, 1, f("h2"))
+        layer(1)
+        if r == 1:
+            vertices(1, 2, 1, None)
+        away(0)
+        made(1, "ssss")
+        both(2)
+        layer(2)
+        away(1)
         if not last:
-            choices_a(r + 1)
-        for b in range(4):
-            tt(il(N, 0, C, b), ind(f("dp", b * C, b * C + C), f("lu")), il(X, 0, C, b), add)
-    xq, xp = "xq%d" % ROUNDS, "xp%d" % ROUNDS
-    quant(f(xq), f(xp), f("x%d" % ROUNDS))
-    for s in range(2):
-        mm(bank(s, HV), f("vq"), f("vpl"), f(xq, HV * s, HV * s + HV), f(xp, HV * s, HV * s + HV))
-    store("y", "oc", T.oc[:, :], T[xq][:, :].bitcast(dt.uint8), f(xq)[1])
-    for k in range(4):
-        store("y", "os%d" % k, T.osc[4 * k:4 * k + 4, :], T[xp][32 * k:32 * k + 4, :], f(xp)[1])
-    act(f("yt", 0, HV), bank(0, HV))
-    cp(f("yt", HV, C), bank(1, HV))
-    store("s", "oy0", T.y[:, 0:HV], T.yt[:, 0:HV], f("yt", 0, HV)[1])
-    store("y", "oy1", T.y[:, HV:C], T.yt[:, HV:C], f("yt", HV, C)[1])
+            places(0, r + 1)
+        if r == 0:
+            quant(f("eq", 256, 512), f("ep", 256, 512), f("eb", 1024, 2048))
+        made(2, "vsvs")
+        away(2)
+
+        def unpack(n, engs):
+            a, b = RUNS[LAND[n][0]][0], RUNS[LAND[n][-1]][1]
+            o = wide((a, b))[0]
+            for e in range(4):
+                i = 4 * ((n + 1) % 2) + e
+                mm(bank(i, 0, b - o), f("eq", 128 * e, 128 * e + 128), f("ep", 128 * e, 128 * e + 128), f(lq, o, b), f(lp, o, b))
+                move(engs[e], il("dp", a, b, e), bank(i, a - o, b - o))
+
+        act(f("lf"), ind(f("ff"), f(rcv)))
+        if not last:
+            scatter(f("fi"), f(rcv))
+            unpack(0, "ssss")
+            act(f("raw"), ind(f("fi"), f("nl%d" % r)))
+            own(4, "sc", "lf")
+            places(1, r + 1)
+            whole4("l4", "sc")
+            places(2, r + 1)
+            unpack(1, "vvvs")
+            sort_slots(r + 2, f("raw", 0, HV), f("raw", HV, C))
+            places(3, r + 1)
+            own(16, "sa", "lh%d" % (r + 2))
+            places(4, r + 1)
+            whole16("nl%d" % (r + 2), "sa")
+        else:
+            own(4, "sc", "lf")
+            quant(f("vq"), f("vpl"), f("vt"))
+            whole4("l4", "sc")
+            unpack(0, "vvvv")
+            affine(f("tpf"), ind(f("hx2"), f(rcv)), 1.0, float(HV))
+            store("y", "otp", T.tp[:, :], T.tpf[0:128:16, :], f("tpf")[1])
+            unpack(1, "svsv")
+        unpack(2, "svsv")
+        for i, run in enumerate(MEET):
+            a, b = run
+            end = i == len(MEET) - 1
+            tt(f(N, 4 * a, 4 * b), ind(f("dp"), f("l4", a // 4, b // 4)), f(X, 4 * a, 4 * b), add)
+            codes_x(r + 1, run)
+            if not last:
+                scores(r + 1, run, i)
+                if r == 0 and i == 0:
+                    act(f("hx2"), ind(f("hx0"), f(rcv)))
+                if not end:
+                    halve("s", r + 1, run)
+                    for k in range(2):
+                        keep_score("s", run, i, k)
+                else:
+                    halve("v", r + 1, run)
+                    keep_score("s", run, i, 0)
+                    out_edges(0, r + 1)
+                    keep_score("v", run, i, 1)
+                    for step in range(2):
+                        out_edges(1 + step, r + 1)
+            else:
+                o, w = wide(run), kept(MEET, i)
+                mm(bank(i, 0, o[1] - o[0]), f("vq"), f("vpl"), f("xq%d" % ROUNDS, o[0], o[1]), f("xp%d" % ROUNDS, o[0], o[1]))
+                store("y", "oc%d" % i, T.oc[:, 4 * w[0]:4 * w[1]], T["xq%d" % ROUNDS][:, w[0]:w[1]].bitcast(dt.uint8), f("xq%d" % ROUNDS, w[0], w[1])[1])
+                if end:
+                    for k in range(4):
+                        store("y", "os%d" % k, T.osc[4 * k:4 * k + 4, :], T["xp%d" % ROUNDS][32 * k:32 * k + 4, :], f("xp%d" % ROUNDS)[1])
+                move("v" if end else "s", f("yt", a, b), bank(i, a - o[0], b - o[0]))
+                store("s", "oy%d" % i, T.y[:, a:b], T.yt[:, a:b], f("yt", a, b)[1])
     for s in cnt:
         if seen["y"].get(s, 0) < cnt[s]:
             g.sync.wait_ge(T.sem[s], cnt[s])

@@ -6,7 +6,9 @@ HV = 176
 ROUNDS = 3
 STEP = (4, 1, 2)
 RUNS = ((0, 128), (128, 256), (256, 352))
-MEET = ((0, 128), (128, 256), (256, 352))
+MEET = ((0, 224), (224, 352))
+HALVES = (144, 240)
+CUT = 10
 LAND = ((0,), (1,), (2,))
 WIDE = 128
 
@@ -66,8 +68,8 @@ _pack("bw", "bfloat16", [(_n, C) for _n in ("io", "w16", "w4", "m0f", "m1f", "ff
       [("lh%d" % _i, C) for _i in _LISTS] + [("by%d" % _i, C) for _i in range(2)] + [("%s%d" % (_n, _k), HV) for _n in ("ci", "co") for _k in range(2)] +
       [("%s%d" % (_n, _k), 3 * HV) for _n in ("sw", "mt") for _k in range(2)])
 _pack("iw", "int32", [(_n, K) for _n in ("ic", "iq", "h2")] + [("vi", 3 * K), ("i4", 2), ("uoi", 16)])
-_pack("uw", "uint16", [("hu", 2 * K), ("vu", 3 * K), ("ks", K), ("uo", 16), ("m16", K)] + [("pu%d" % _i, K) for _i in range(ROUNDS)] +
-      [("nl%d" % _i, K) for _i in _LISTS] + [(_n, 4 * K) for _n in ("m4", "f4", "l4")])
+_pack("uw", "uint16", [("hu", 2 * K), ("vu", 3 * K), ("ks", K), ("uo", 16), ("m16", K), ("l16", K)] + [("pu%d" % _i, K) for _i in range(ROUNDS)] +
+      [("nl%d" % _i, K) for _i in _LISTS] + [(_n, 4 * K) for _n in ("m4", "f4")])
 for _i in range(8):
     _buf("b%d" % _i, 512, "float32", "psum")
 
@@ -226,8 +228,8 @@ def rank_program(g, core, T, topo):
     iota(f("ic"), [[0, K]], 0, 1, False)
     iota(f("j16"), [[1, 16]], 0, 0)
     iota(f("j4"), [[0, 4], [1, 4]], 0, 0)
-    iota(f("io"), [[1, C]], -HV, 0)
     iota(f("uoi"), [[1, 2], [16, 8]], 0, 0, False)
+    iota(f("io"), [[1, C]], -HV, 0)
     iota(f("e16", 0, K), [[16, K]], -HV, 0)
     for k in range(2):
         iota(third("sw%d" % k, 0), [[0, HV]], 0, 0)
@@ -263,9 +265,9 @@ def rank_program(g, core, T, topo):
     def hi(i):
         return f("nl%d" % i, K // 2 - 1, K)
 
-    def scatter(win, lst):
+    def scatter(win, lst, e):
         o = ind(win, lst)
-        emit("v", lambda: g.vector.tensor_copy(o[0], f("io")[0]), lst[1] + f("io")[1], win[1])
+        emit("v", lambda: g.vector.tensor_copy(o[0], e[0]), lst[1] + e[1], win[1])
 
     def sort_slots(i, a, b):
         tt(f("lh%d" % i, 0, HV), a, b, AluOpType.min)
@@ -279,9 +281,9 @@ def rank_program(g, core, T, topo):
             cp(f("vu", a, b), f("vi", a, b))
             ts(f("v3", a, b), f("vi", a, b), 3, mult, 1, add)
 
-    def places(step, i):
+    def places(step, i, a=0, b=K):
         if step == 0:
-            act(f("he"), ind(f("lh%d" % i, HV, C), f("vu", K * i, K * i + K)))
+            act(f("he", 16 * a, 16 * b), ind(f("lh%d" % i, HV, C), f("vu", K * i + a, K * i + b)))
         elif step == 1:
             own(16, "sb", "he")
         elif step == 2:
@@ -313,8 +315,8 @@ def rank_program(g, core, T, topo):
         a = wide(run)[0]
         move(eng, f("s%d" % k, run[0], run[1]), bank(2 * i + k, run[0] - a, run[1] - a))
 
-    def halve(eng, r, run):
-        move(eng, f("xh", 4 * run[0], 4 * run[1]), f("x%d" % r, 4 * run[0], 4 * run[1]), 0.5)
+    def halve(eng, r, a, b):
+        move(eng, f("xh", 4 * a, 4 * b), f("x%d" % r, 4 * a, 4 * b), 0.5)
 
     def second(k, side, i):
         act(f("h%s%d" % (side, k)), ind(f("s%d" % k), hi(i)))
@@ -328,23 +330,23 @@ def rank_program(g, core, T, topo):
     def table(k):
         scan(f("mt%d" % k), f("sw%d" % k), f("ends"), mult, add)
 
+    cp(f("uo"), f("uoi"))
     cp(f("hu"), f("hlt"))
     vertices(0, 0, 2, f("hlt"))
-    scatter(f("by0"), f("hu", 0, K))
+    scatter(f("by0"), f("hu", 0, K), f("io"))
     act(f("hx0"), ind(f("io"), f("hu", 0, K)))
     vertices(1, 0, 2, None)
     sort_slots(0, f("by0", 0, C, 2), f("by0", 1, C, 2))
     quant(f("uq"), f("up"), f("ut"))
-    cp(f("uo"), f("uoi"))
     own(16, "sa", "lh0")
     cp(u32(f("uk")), ind(u32(f("uq")), f("uo")))
     act(f("ukp"), ind(f("up"), f("uo")))
     places(0, 0)
-    halve("s", 0, RUNS[0])
+    halve("s", 0, 0, HALVES[0])
     whole16("nl0", "sa")
     codes_x(0, (0, C))
     scores(0, (0, C), 0)
-    scatter(f("by1"), f("hu", K, 2 * K))
+    scatter(f("by1"), f("hu", K, 2 * K), f("io"))
     for k in range(2):
         keep_score("s", (0, C), 0, k)
         second(k, "i", 0)
@@ -377,19 +379,22 @@ def rank_program(g, core, T, topo):
         if r == 0:
             for k in range(2):
                 second(k, "o", 1)
-            halve("s", 0, (RUNS[0][1], C))
+            halve("s", 0, HALVES[0], C)
             higher(0, "i", r)
             for step in range(3):
                 out_edges(step, r)
             higher(0, "o", r + 1)
         else:
-            for k in range(2):
-                second(k, "i", r)
-                second(k, "o", r + 1)
+            second(0, "i", r)
+            cp(f("ho0"), ind(f("s0"), hi(r + 1)))
+            keep_score("s", MEET[-1], len(MEET) - 1, 1)
+            second(1, "i", r)
+            second(1, "o", r + 1)
+            halve("s", r, 0, HALVES[0])
             higher(0, "i", r)
             higher(0, "o", r + 1)
-        higher(1, "i", r)
         crossed(0)
+        higher(1, "i", r)
         table(0)
         onward(0)
         higher(1, "o", r + 1)
@@ -402,9 +407,20 @@ def rank_program(g, core, T, topo):
         whole16("m16", "sd")
         if r == 0:
             quant(f("eq", 0, 256), f("ep", 0, 256), f("eb", 0, 1024))
-        if r == 1:
-            own(16, "sb", "hx2")
-            whole16("h2", "sb")
+        else:
+            halve("v", r, HALVES[0], HALVES[1])
+
+        def heads(only, step):
+            if r != only:
+                return
+            if r == 0:
+                places(step + 1, 1)
+            elif step == 0:
+                own(16, "sb", "hx2")
+            elif step == 1:
+                whole16("h2", "sb")
+            else:
+                vertices(step - 2, 2, 1, f("h2"))
 
         def first(i):
             a, b = RUNS[i]
@@ -447,77 +463,113 @@ def rank_program(g, core, T, topo):
         both(0)
         layer(0)
         first(2)
+        if r == 0:
+            places(0, 1, 0, 10)
         made(0, "ssss")
+        if r == 0:
+            places(0, 1, 10, K)
         both(1)
-        if r == 1:
-            vertices(0, 2, 1, f("h2"))
+        heads(1, 0)
         layer(1)
-        if r == 1:
-            vertices(1, 2, 1, None)
+        heads(1, 1)
         away(0)
         made(1, "ssss")
         both(2)
+        heads(1, 2)
         layer(2)
+        heads(1, 3)
         away(1)
-        if not last:
-            places(0, r + 1)
         if r == 0:
             quant(f("eq", 256, 512), f("ep", 256, 512), f("eb", 1024, 2048))
-        made(2, "vsvs")
+        if not last:
+            scatter(f("fi"), f(rcv, 0, CUT), f("io", 0, 16 * CUT))
+        made(2, "vsvs" if last else "ssss")
         away(2)
 
-        def unpack(n, engs):
+        def landed(n):
             a, b = RUNS[LAND[n][0]][0], RUNS[LAND[n][-1]][1]
-            o = wide((a, b))[0]
+            return a, b, wide((a, b))[0], 4 * ((n + len(RUNS)) % 2)
+
+        def products(n):
+            a, b, o, i = landed(n)
             for e in range(4):
-                i = 4 * ((n + 1) % 2) + e
-                mm(bank(i, 0, b - o), f("eq", 128 * e, 128 * e + 128), f("ep", 128 * e, 128 * e + 128), f(lq, o, b), f(lp, o, b))
-                move(engs[e], il("dp", a, b, e), bank(i, a - o, b - o))
+                mm(bank(i + e, 0, b - o), f("eq", 128 * e, 128 * e + 128), f("ep", 128 * e, 128 * e + 128), f(lq, o, b), f(lp, o, b))
+
+        def keep(n, engs, e0):
+            a, b, o, i = landed(n)
+            for e, eng in enumerate(engs, e0):
+                move(eng, f("dp", e * C + a, e * C + b), bank(i + e, a - o, b - o))
+
+        def unpack(n, engs):
+            products(n)
+            keep(n, engs, 0)
 
         act(f("lf"), ind(f("ff"), f(rcv)))
         if not last:
-            scatter(f("fi"), f(rcv))
-            unpack(0, "ssss")
+            scatter(f("fi"), f(rcv, CUT, K), f("io", 16 * CUT, C))
+            products(0)
+            keep(0, "ss", 0)
             act(f("raw"), ind(f("fi"), f("nl%d" % r)))
-            own(4, "sc", "lf")
-            places(1, r + 1)
-            whole4("l4", "sc")
-            places(2, r + 1)
-            unpack(1, "vvvs")
+            own(16, "sc", "lf")
+            keep(0, "v", 2)
+            whole16("l16", "sc")
+            keep(0, "v", 3)
+            heads(0, 0)
+            unpack(1, "ssss")
             sort_slots(r + 2, f("raw", 0, HV), f("raw", HV, C))
-            places(3, r + 1)
+            heads(0, 1)
             own(16, "sa", "lh%d" % (r + 2))
-            places(4, r + 1)
+            out_edges(0, r + 1)
             whole16("nl%d" % (r + 2), "sa")
+            heads(0, 2)
+            out_edges(1, r + 1)
+            heads(0, 3)
+            out_edges(2, r + 1)
         else:
-            own(4, "sc", "lf")
+            own(16, "sc", "lf")
             quant(f("vq"), f("vpl"), f("vt"))
-            whole4("l4", "sc")
+            whole16("l16", "sc")
             unpack(0, "vvvv")
             affine(f("tpf"), ind(f("hx2"), f(rcv)), 1.0, float(HV))
             store("y", "otp", T.tp[:, :], T.tpf[0:128:16, :], f("tpf")[1])
             unpack(1, "svsv")
-        unpack(2, "svsv")
+        unpack(2, "ssss")
+
+        def meet(e, a, b):
+            tt(il(N, a, b, e), ind(f("dp", e * C, e * C + C), f("l16", a // 16, b // 16)), il(X, a, b, e), add)
+
+        a, b = MEET[-1]
+        for e in range(4):
+            act(il("at", a, b, e), ind(f("dp", e * C, e * C + C), f("l16", a // 16, b // 16)))
+        if r == 0:
+            act(f("hx2"), ind(f("hx0"), f(rcv)))
+        if r == 1:
+            places(0, 2)
         for i, run in enumerate(MEET):
             a, b = run
             end = i == len(MEET) - 1
-            tt(f(N, 4 * a, 4 * b), ind(f("dp"), f("l4", a // 4, b // 4)), f(X, 4 * a, 4 * b), add)
+            if end:
+                tt(f(N, 4 * a, 4 * b), f("at", 4 * a, 4 * b), f(X, 4 * a, 4 * b), add)
+                if r == 1:
+                    places(1, 2)
+            else:
+                for e in range(4):
+                    meet(e, a, b)
             codes_x(r + 1, run)
             if not last:
                 scores(r + 1, run, i)
-                if r == 0 and i == 0:
-                    act(f("hx2"), ind(f("hx0"), f(rcv)))
                 if not end:
-                    halve("s", r + 1, run)
                     for k in range(2):
                         keep_score("s", run, i, k)
                 else:
-                    halve("v", r + 1, run)
-                    keep_score("s", run, i, 0)
-                    out_edges(0, r + 1)
-                    keep_score("v", run, i, 1)
-                    for step in range(2):
-                        out_edges(1 + step, r + 1)
+                    if r == 1:
+                        places(2, 2)
+                    halve("v", r + 1, HALVES[1], C)
+                    if r == 1:
+                        places(3, 2)
+                    keep_score("v", run, i, 0)
+                    if r == 1:
+                        places(4, 2)
             else:
                 o, w = wide(run), kept(MEET, i)
                 mm(bank(i, 0, o[1] - o[0]), f("vq"), f("vpl"), f("xq%d" % ROUNDS, o[0], o[1]), f("xp%d" % ROUNDS, o[0], o[1]))

from concourse.mybir import dt, AluOpType, ActivationFunctionType

C = 352
K = 22
HV = 176
ROUNDS = 3
STEP = (4, 1, 2)
RUNS = ((0, 128), (128, 256), (256, 352))
MEET = ((0, 224), (224, 352))
HALVES = (144, 240)
CUT = 10
LAND = ((0,), (1,), (2,))
WIDE = 128


def wide(run):
    return (min(run[0], run[1] - WIDE), run[1])


def kept(runs, i):
    return (wide(runs[i])[0] if i else 0, wide(runs[i + 1])[0] if i + 1 < len(runs) else C)


SLOT = [0]
for _run in RUNS:
    SLOT.append(SLOT[-1] + _run[1] - wide(_run)[0])

SCRATCH = {}
LOC = {}


def _buf(name, cols, dtype, where="sbuf"):
    SCRATCH[name] = (where, [128, cols], dtype)
    LOC[name] = (name, 0, cols)


def _pack(name, dtype, parts):
    n = 0
    for part, cols in parts:
        LOC[part] = (name, n, cols)
        n += cols
    SCRATCH[name] = ("sbuf", [128, n], dtype)


for _r in range(ROUNDS + 1):
    _buf("x%d" % _r, 4 * C, "bfloat16")
    _buf("xq%d" % _r, C, "float8_e4m3fn_x4")
    _buf("xp%d" % _r, C, "uint8")
for _r in range(ROUNDS):
    _buf("hq%d" % _r, SLOT[-1], "float8_e4m3fn_x4")
    _buf("hp%d" % _r, SLOT[-1], "uint8")
    _buf("lq%d" % _r, C, "float8_e4m3fn_x4")
    _buf("lp%d" % _r, C, "uint8")
    _buf("snd%d" % _r, K, "uint16")
    _buf("rcv%d" % _r, K, "uint16")
for _n, _c, _t in (("xh", 4 * C, "bfloat16"), ("at", 4 * C, "bfloat16"), ("zt", 4 * C, "bfloat16"), ("zq", SLOT[-1], "float8_e4m3fn_x4"), ("zp", SLOT[-1], "uint8"),
                   ("ht", 4 * C, "bfloat16"), ("dp", 4 * C, "bfloat16"), ("one", 512, "bfloat16"), ("eb", 2048, "bfloat16"),
                   ("eq", 512, "float8_e4m3fn_x4"), ("ep", 512, "uint8"), ("ut", 512, "bfloat16"), ("vt", 512, "bfloat16"),
                   ("uq", 128, "float8_e4m3fn_x4"), ("up", 128, "uint8"), ("uk", 256, "float8_e4m3fn_x4"), ("ukp", 256, "uint8"),
                   ("vq", 128, "float8_e4m3fn_x4"), ("vpl", 128, "uint8"), ("wq", 512, "float8_e4m3fn_x4"), ("wpl", 512, "uint8"),
                   ("hlt", 2 * K, "int32"), ("yt", C, "float32"), ("tpf", C, "float32"), ("ends", 3 * HV, "float16")):
    _buf(_n, _c, _t)
_LISTS = range(ROUNDS + 1)
_pack("fw", "float32", [("s0", C), ("s1", C)] + [("%s%d" % (_n, _k), HV + 16) for _n in ("hi", "ho") for _k in range(2)] +
      [(_n, 16) for _n in ("j16", "j4", "ge16", "eq16", "ge4", "eq4", "t16", "t4")] + [(_n, 8) for _n in ("qf", "q4", "q3", "c4", "qh")] +
      [(_n, 24) for _n in ("e16", "ewc", "bit", "p3")] + [("v3", 3 * K + 6)])
_pack("bw", "bfloat16", [(_n, C) for _n in ("io", "w16", "w4", "m0f", "m1f", "ff", "lf", "fi", "raw", "he", "hx0", "hx2", "sa", "sb", "sc", "sd")] +
      [("lh%d" % _i, C) for _i in _LISTS] + [("by%d" % _i, C) for _i in range(2)] + [("%s%d" % (_n, _k), HV) for _n in ("ci", "co") for _k in range(2)] +
      [("%s%d" % (_n, _k), 3 * HV) for _n in ("sw", "mt") for _k in range(2)])
_pack("iw", "int32", [(_n, K) for _n in ("ic", "iq", "h2")] + [("vi", 3 * K), ("i4", 2), ("uoi", 16)])
_pack("uw", "uint16", [("hu", 2 * K), ("vu", 3 * K), ("ks", K), ("uo", 16), ("m16", K), ("l16", K)] + [("pu%d" % _i, K) for _i in range(ROUNDS)] +
      [("nl%d" % _i, K) for _i in _LISTS] + [(_n, 4 * K) for _n in ("m4", "f4")])
for _i in range(8):
    _buf("b%d" % _i, 512, "float32", "psum")

SEMAPHORES = ["qv", "qs", "qt", "qg", "ldh", "ldt", "ldx", "ldu", "ldv", "ldw", "lds", "otp", "os0", "os1", "os2", "os3"]
SEMAPHORES += ["%s%d" % (_n, _i) for _n in ("oy", "oc") for _i in range(len(MEET))]
for _r in range(ROUNDS):
    for _n in ["l"] + ["q%d" % _i for _i in range(len(RUNS))] + ["p%d" % _i for _i in range(len(LAND))]:
        SEMAPHORES += ["r%s%d" % (_n, _r), "l%s%d" % (_n, _r)]


def rank_program(g, core, T, topo):
    rank = T.rank_of(core)
    if rank is None:
        return
    queue = {"v": g.vector, "s": g.scalar, "t": g.tensor, "g": g, "y": g.sync}
    seen = {e: {} for e in queue}
    cnt = {}
    acc = {}

    def clash(a, b):
        return a[0] == b[0] and a[1] < b[2] and b[1] < a[2] and (a[3] is None or b[3] is None or a[3] == b[3])

    def emit(eng, fn, reads, writes, sem=None, inc=1, events=None):
        need = {}
        for regs, wr in ((reads, False), (writes, True)):
            for rg in regs:
                for a in acc.get(rg[0], []):
                    if not clash(rg, a[0]):
                        continue
                    if not wr and not a[1] and not (rg[4] and a[2] != eng):
                        continue
                    if seen[eng].get(a[3], 0) < a[4] and need.get(a[3], (0,))[0] < a[4]:
                        need[a[3]] = (a[4], a[5])
        for s in list(need):
            for o in need:
                if o != s and need[o][1].get(s, 0) >= need[s][0]:
                    del need[s]
                    break
        for s in need:
            queue[eng].wait_ge(T.sem[s], need[s][0])
            for o in need[s][1]:
                seen[eng][o] = max(seen[eng].get(o, 0), need[s][1][o])
            seen[eng][s] = need[s][0]
        ins = fn()
        clock = dict(seen[eng])
        if events is None:
            s = sem or "q" + eng
            cnt[s] = cnt.get(s, 0) + inc
            ins.then_inc(T.sem[s], inc)
            ev = (s, cnt[s])
        else:
            for s, n in events:
                cnt[s] = cnt.get(s, 0) + n
            ev = (events[0][0], cnt[events[0][0]])
        for regs, wr in ((reads, False), (writes, True)):
            for rg in regs:
                old = acc.get(rg[0], [])
                if wr:
                    old = [a for a in old if not (rg[1] <= a[0][1] and a[0][2] <= rg[2] and (rg[3] is None or rg[3] == a[0][3]))]
                old.append((rg, wr, eng, ev[0], ev[1], clock))
                acc[rg[0]] = old

    def f(name, a=0, b=None, step=1):
        buf, off, n = LOC[name]
        a, b = off + a, off + (n if b is None else b)
        return (T[buf][:, a:b:step] if step > 1 else T[buf][:, a:b], [(buf, a, b, None, False)])

    def third(name, e):
        buf, off, n = LOC[name]
        return (T[buf][:, off + e:off + n:3], [(buf, off, off + n, e, False)])

    def il(name, a, b, e):
        return (T[name][:, 4 * a + e:4 * b:4], [(name, 4 * a, 4 * b, e, False)])

    def bank(i, a, b):
        return (T["b%d" % i][:, a:b], [("b%d" % i, 0, 512, None, True)])

    def ind(win, off):
        return (win[0].indirect(off[0]), win[1] + off[1])

    def u32(v):
        return (v[0].bitcast(dt.uint32), v[1])

    def tt(out, a, b, op):
        emit("v", lambda: g.vector.tensor_tensor(out[0], a[0], b[0], op), a[1] + b[1], out[1])

    def ts(out, a, c1, op0, c2=None, op1=None, col=None):
        if op1 is None:
            emit("v", lambda: g.vector.tensor_scalar(out[0], a[0], c1, None, op0), a[1] + (col or []), out[1])
        else:
            emit("v", lambda: g.vector.tensor_scalar(out[0], a[0], c1, c2, op0, op1), a[1] + (col or []), out[1])

    def cp(out, a):
        emit("v", lambda: g.vector.tensor_copy(out[0], a[0]), a[1], out[1])

    def act(out, a, scale=None):
        if scale is None:
            emit("s", lambda: g.scalar.activation(out[0], a[0], ActivationFunctionType.Copy), a[1], out[1])
        else:
            emit("s", lambda: g.scalar.activation(out[0], a[0], ActivationFunctionType.Copy, scale=scale), a[1], out[1])

    def affine(out, a, scale, bias, col=None):
        emit("s", lambda: g.scalar.activation(out[0], a[0], ActivationFunctionType.Identity, bias=bias, scale=scale), a[1] + (col or []), out[1])

    def move(eng, out, a, scale=None):
        if eng == "s":
            act(out, a, scale)
        elif scale is None:
            cp(out, a)
        else:
            ts(out, a, scale, AluOpType.mult)

    def scan(out, a, w, op0=AluOpType.add, op1=AluOpType.mult):
        emit("v", lambda: g.vector.tensor_tensor_scan(out[0], a[0], w[0], 0.0, op0, op1), a[1] + w[1], out[1])

    def quant(codes, plane, src):
        emit("v", lambda: g.vector.quantize_mx(codes[0], plane[0], src[0]), src[1], codes[1] + plane[1])

    def mm(out, w, ws, m, ms):
        emit("t", lambda: g.tensor.matmul_mx(out[0], w[0], ws[0], m[0], ms[0], True, True), w[1] + ws[1] + m[1] + ms[1], out[1])

    def iota(out, pattern, base, cm, imprecise=True):
        if imprecise:
            emit("g", lambda: g.iota(out[0], pattern, base, cm, allow_small_or_imprecise_dtypes=True), [], out[1])
        else:
            emit("g", lambda: g.iota(out[0], pattern, base, cm), [], out[1])

    def load(eng, sem, name, src, a=0, b=None, codes=False):
        o = f(name, a, b)
        emit(eng, lambda: queue[eng].dma_start(o[0].bitcast(dt.uint8) if codes else o[0], src[:, :]), [], o[1], sem=sem, inc=16)

    def store(eng, sem, dst, src, regs):
        emit(eng, lambda: queue[eng].dma_start(dst, src), regs, [], sem=sem, inc=16)

    add, sub, mult = AluOpType.add, AluOpType.subtract, AluOpType.mult
    BIG, LS = 16, 15

    def own(n, scr, flat):
        scan(f(scr), f(flat), f("w%d" % n))

    def whole16(out, scr):
        ts(f(out), f(scr, 15, C, 16), 2.0 ** LS, mult, HV + 0.25, add)

    def whole4(out, scr):
        c4 = f("c4", 0, 1)
        ts(f(out), f(scr, 3, C, 4), 2.0 ** (LS + 2), mult, c4[0], add, col=c4[1])

    load("y", "ldh", "hlt", T.hl, 0, K)
    load("s", "ldt", "hlt", T.tl, K, 2 * K)
    load("y", "ldu", "ut", T.u)
    load("y", "ldx", "x0", T.x)
    load("y", "ldw", "wq", T.wc, codes=True)
    load("y", "lds", "wpl", T.ws)
    load("y", "ldv", "vt", T.v)

    iota(f("ic"), [[0, K]], 0, 1, False)
    iota(f("j16"), [[1, 16]], 0, 0)
    iota(f("j4"), [[0, 4], [1, 4]], 0, 0)
    iota(f("uoi"), [[1, 2], [16, 8]], 0, 0, False)
    iota(f("io"), [[1, C]], -HV, 0)
    iota(f("e16", 0, K), [[16, K]], -HV, 0)
    for k in range(2):
        iota(third("sw%d" % k, 0), [[0, HV]], 0, 0)
        iota(third("sw%d" % k, 2), [[0, HV]], -1, 0)
    iota(f("one"), [[0, 512]], 1, 0)
    for b in range(4):
        o = f("eb", 512 * b, 512 * b + 512)
        emit("g", lambda: g.affine_select(o[0], T.one[:, :], [[-1, 512]], AluOpType.is_equal, 0.0, b, 4), f("one")[1], o[1])
    ts(f("iq"), f("ic"), 15, AluOpType.bitwise_and)
    cp(f("qf", 0, 2), f("iq", 0, 2))
    ts(f("i4"), f("iq", 0, 2), 2, AluOpType.arith_shift_right)
    cp(f("ks"), f("iq"))
    cp(f("q4", 0, 2), f("i4"))
    qf, q4 = f("qf", 0, 1), f("q4", 0, 1)
    tabs = ((16, qf), (4, q4))
    for n, at in tabs:
        ts(f("ge%d" % n), f("j%d" % n), at[0], AluOpType.is_ge, col=at[1])
        ts(f("eq%d" % n), f("j%d" % n), at[0], AluOpType.is_equal, 2.0 ** BIG - 1.0, mult, col=at[1])
    for n, at in tabs:
        tt(f("t%d" % n), f("eq%d" % n), f("ge%d" % n), add)
    for n, at in tabs:
        ts(f("t%d" % n, n - 1, 16, n), f("t%d" % n, n - 1, 16, n), 2.0 ** (-BIG - LS), mult)
    affine(f("q3", 0, 1), q4, -4.0, qf[0], qf[1])
    affine(f("qh", 0, 1), qf, 2.0 ** -LS, 2.0 ** (-LS - 1))
    affine(f("c4", 0, 1), f("q3", 0, 1), 1.0, 4 * HV + 0.25)
    for n, at in tabs:
        act(f("w%d" % n), ind(f("t%d" % n), f("ks")))
    affine(f("ewc", 0, K), f("e16", 0, K), 2.0 ** -LS, f("qh", 0, 1)[0], f("qh", 0, 1)[1])

    def lo(i):
        return f("nl%d" % i, 0, K // 2)

    def hi(i):
        return f("nl%d" % i, K // 2 - 1, K)

    def scatter(win, lst, e):
        o = ind(win, lst)
        emit("v", lambda: g.vector.tensor_copy(o[0], e[0]), lst[1] + e[1], win[1])

    def sort_slots(i, a, b):
        tt(f("lh%d" % i, 0, HV), a, b, AluOpType.min)
        tt(f("lh%d" % i, HV, C), a, b, AluOpType.max)

    def vertices(step, i, n, src):
        a, b = K * i, K * (i + n)
        if step == 0:
            ts(f("vi", a, b), src, 1, AluOpType.arith_shift_right)
        else:
            cp(f("vu", a, b), f("vi", a, b))
            ts(f("v3", a, b), f("vi", a, b), 3, mult, 1, add)

    def places(step, i, a=0, b=K):
        if step == 0:
            act(f("he", 16 * a, 16 * b), ind(f("lh%d" % i, HV, C), f("vu", K * i + a, K * i + b)))
        elif step == 1:
            own(16, "sb", "he")
        elif step == 2:
            tt(f("bit", 0, K), f("sb", 15, C, 16), f("ewc", 0, K), AluOpType.is_lt)
        elif step == 3:
            tt(f("p3", 0, K), f("bit", 0, K), f("v3", K * i, K * i + K), add)
        else:
            cp(f("pu%d" % i), f("p3", 0, K))

    def out_edges(step, r):
        a, b = f("lh%d" % (r + 1), 0, HV), f("lh%d" % (r + 1), HV, C)
        if step == 0:
            tt(third("ends", 0), b, a, sub)
        elif step == 1:
            cp(third("ends", 1), a)
        else:
            tt(third("ends", 2), b, a, add)

    def codes_x(r, run):
        a, b = wide(run)
        quant(f("xq%d" % r, a, b), f("xp%d" % r, a, b), f("x%d" % r, 4 * a, 4 * b))

    def scores(r, run, i):
        a, b = wide(run)
        for k in range(2):
            mm(bank(2 * i + k, 0, b - a), f("uk", 128 * k, 128 * k + 128), f("ukp", 128 * k, 128 * k + 128), f("xq%d" % r, a, b), f("xp%d" % r, a, b))

    def keep_score(eng, run, i, k):
        a = wide(run)[0]
        move(eng, f("s%d" % k, run[0], run[1]), bank(2 * i + k, run[0] - a, run[1] - a))

    def halve(eng, r, a, b):
        move(eng, f("xh", 4 * a, 4 * b), f("x%d" % r, 4 * a, 4 * b), 0.5)

    def second(k, side, i):
        act(f("h%s%d" % (side, k)), ind(f("s%d" % k), hi(i)))

    def higher(k, side, i):
        tt(f("c%s%d" % (side, k)), ind(f("s%d" % k), lo(i)), f("h%s%d" % (side, k), 16), AluOpType.is_ge)

    def crossed(k):
        tt(third("sw%d" % k, 1), f("ci%d" % k), f("co%d" % k), AluOpType.not_equal)

    def table(k):
        scan(f("mt%d" % k), f("sw%d" % k), f("ends"), mult, add)

    cp(f("uo"), f("uoi"))
    cp(f("hu"), f("hlt"))
    vertices(0, 0, 2, f("hlt"))
    scatter(f("by0"), f("hu", 0, K), f("io"))
    act(f("hx0"), ind(f("io"), f("hu", 0, K)))
    vertices(1, 0, 2, None)
    sort_slots(0, f("by0", 0, C, 2), f("by0", 1, C, 2))
    quant(f("uq"), f("up"), f("ut"))
    own(16, "sa", "lh0")
    cp(u32(f("uk")), ind(u32(f("uq")), f("uo")))
    act(f("ukp"), ind(f("up"), f("uo")))
    places(0, 0)
    halve("s", 0, 0, HALVES[0])
    whole16("nl0", "sa")
    codes_x(0, (0, C))
    scores(0, (0, C), 0)
    scatter(f("by1"), f("hu", K, 2 * K), f("io"))
    for k in range(2):
        keep_score("s", (0, C), 0, k)
        second(k, "i", 0)
    places(1, 0)
    sort_slots(1, f("by1", 0, C, 2), f("by1", 1, C, 2))
    places(2, 0)
    own(16, "sa", "lh1")
    places(3, 0)
    whole16("nl1", "sa")
    places(4, 0)

    def send(r, src, a, dst, c, d, sem, codes=False):
        to = T.cores[rank ^ STEP[r]]
        rid, pid = topo.addr(to, core)
        n = len(topo.engines(core, to))
        rs, ls = "r%s%d" % (sem, r), "l%s%d" % (sem, r)
        view = (lambda v: v.bitcast(dt.uint8)) if codes else (lambda v: v)
        emit("g", lambda: g.remote_dma(view(T[dst][:, c:d]), view(T[src][:, a:a + d - c]), T.sem[rs], T.sem[ls], pid, rid, topo.mask(core, to)),
             f(src, a, a + d - c)[1], [], events=[(ls, n)])
        cnt[rs] = n
        acc.setdefault(dst, []).append(((dst, c, d, None, False), True, "far", rs, n, {}))

    for r in range(ROUNDS):
        X, N, last = "x%d" % r, "x%d" % (r + 1), r == ROUNDS - 1
        hq, hp, lq, lp, snd, rcv = ["%s%d" % (n, r) for n in ("hq", "hp", "lq", "lp", "snd", "rcv")]

        def onward(k):
            act(f("m%df" % k), ind(f("mt%d" % k), f("pu%d" % r)))

        if r == 0:
            for k in range(2):
                second(k, "o", 1)
            halve("s", 0, HALVES[0], C)
            higher(0, "i", r)
            for step in range(3):
                out_edges(step, r)
            higher(0, "o", r + 1)
        else:
            second(0, "i", r)
            cp(f("ho0"), ind(f("s0"), hi(r + 1)))
            keep_score("s", MEET[-1], len(MEET) - 1, 1)
            second(1, "i", r)
            second(1, "o", r + 1)
            halve("s", r, 0, HALVES[0])
            higher(0, "i", r)
            higher(0, "o", r + 1)
        crossed(0)
        higher(1, "i", r)
        table(0)
        onward(0)
        higher(1, "o", r + 1)
        crossed(1)
        table(1)
        onward(1)
        own(4, "sc", "m0f")
        own(16, "sd", "m0f")
        whole4("m4", "sc")
        whole16("m16", "sd")
        if r == 0:
            quant(f("eq", 0, 256), f("ep", 0, 256), f("eb", 0, 1024))
        else:
            halve("v", r, HALVES[0], HALVES[1])

        def heads(only, step):
            if r != only:
                return
            if r == 0:
                places(step + 1, 1)
            elif step == 0:
                own(16, "sb", "hx2")
            elif step == 1:
                whole16("h2", "sb")
            else:
                vertices(step - 2, 2, 1, f("h2"))

        def first(i):
            a, b = RUNS[i]
            act(f("at", 4 * a, 4 * b), ind(f(X), f("m4", a // 4, b // 4)), 0.5)

        def both(i):
            a, b = RUNS[i]
            tt(f("zt", 4 * a, 4 * b), ind(f("xh"), f("f4", a // 4, b // 4)), f("at", 4 * a, 4 * b), add)

        def layer(i):
            a, b = wide(RUNS[i])
            zq, zp = f("zq", SLOT[i], SLOT[i + 1]), f("zp", SLOT[i], SLOT[i + 1])
            quant(zq, zp, f("zt", 4 * a, 4 * b))
            for e in range(4):
                mm(bank(4 * (i % 2) + e, 0, b - a), f("wq", 128 * e, 128 * e + 128), f("wpl", 128 * e, 128 * e + 128), zq, zp)

        def made(i, engs):
            a, b = RUNS[i]
            o = wide(RUNS[i])[0]
            for e in range(4):
                move(engs[e], il("ht", a, b, e), bank(4 * (i % 2) + e, a - o, b - o), 0.03125)

        def away(i):
            a, b = wide(RUNS[i])
            quant(f(hq, SLOT[i], SLOT[i + 1]), f(hp, SLOT[i], SLOT[i + 1]), f("ht", 4 * a, 4 * b))
            send(r, hq, SLOT[i] + RUNS[i][0] - a, lq, RUNS[i][0], b, "q%d" % i, True)
            for n, runs in enumerate(LAND):
                if runs[-1] == i:
                    j = runs[0]
                    send(r, hp, SLOT[j] + RUNS[j][0] - wide(RUNS[j])[0], lp, RUNS[j][0], b, "p%d" % n)

        first(0)
        cp(f("ff"), ind(f("m1f"), f("m16")))
        own(4, "sc", "ff")
        own(16, "sd", "ff")
        whole4("f4", "sc")
        whole16(snd, "sd")
        send(r, snd, 0, rcv, 0, K, "l")
        first(1)
        both(0)
        layer(0)
        first(2)
        if r == 0:
            places(0, 1, 0, 10)
        made(0, "ssss")
        if r == 0:
            places(0, 1, 10, K)
        both(1)
        heads(1, 0)
        layer(1)
        heads(1, 1)
        away(0)
        made(1, "ssss")
        both(2)
        heads(1, 2)
        layer(2)
        heads(1, 3)
        away(1)
        if r == 0:
            quant(f("eq", 256, 512), f("ep", 256, 512), f("eb", 1024, 2048))
        if not last:
            scatter(f("fi"), f(rcv, 0, CUT), f("io", 0, 16 * CUT))
        made(2, "vsvs" if last else "ssss")
        away(2)

        def landed(n):
            a, b = RUNS[LAND[n][0]][0], RUNS[LAND[n][-1]][1]
            return a, b, wide((a, b))[0], 4 * ((n + len(RUNS)) % 2)

        def products(n):
            a, b, o, i = landed(n)
            for e in range(4):
                mm(bank(i + e, 0, b - o), f("eq", 128 * e, 128 * e + 128), f("ep", 128 * e, 128 * e + 128), f(lq, o, b), f(lp, o, b))

        def keep(n, engs, e0):
            a, b, o, i = landed(n)
            for e, eng in enumerate(engs, e0):
                move(eng, f("dp", e * C + a, e * C + b), bank(i + e, a - o, b - o))

        def unpack(n, engs):
            products(n)
            keep(n, engs, 0)

        act(f("lf"), ind(f("ff"), f(rcv)))
        if not last:
            scatter(f("fi"), f(rcv, CUT, K), f("io", 16 * CUT, C))
            products(0)
            keep(0, "ss", 0)
            act(f("raw"), ind(f("fi"), f("nl%d" % r)))
            own(16, "sc", "lf")
            keep(0, "v", 2)
            whole16("l16", "sc")
            keep(0, "v", 3)
            heads(0, 0)
            unpack(1, "ssss")
            sort_slots(r + 2, f("raw", 0, HV), f("raw", HV, C))
            heads(0, 1)
            own(16, "sa", "lh%d" % (r + 2))
            out_edges(0, r + 1)
            whole16("nl%d" % (r + 2), "sa")
            heads(0, 2)
            out_edges(1, r + 1)
            heads(0, 3)
            out_edges(2, r + 1)
        else:
            own(16, "sc", "lf")
            quant(f("vq"), f("vpl"), f("vt"))
            whole16("l16", "sc")
            unpack(0, "vvvv")
            affine(f("tpf"), ind(f("hx2"), f(rcv)), 1.0, float(HV))
            store("y", "otp", T.tp[:, :], T.tpf[0:128:16, :], f("tpf")[1])
            unpack(1, "svsv")
        unpack(2, "ssss")

        def meet(e, a, b):
            tt(il(N, a, b, e), ind(f("dp", e * C, e * C + C), f("l16", a // 16, b // 16)), il(X, a, b, e), add)

        a, b = MEET[-1]
        for e in range(4):
            act(il("at", a, b, e), ind(f("dp", e * C, e * C + C), f("l16", a // 16, b // 16)))
        if r == 0:
            act(f("hx2"), ind(f("hx0"), f(rcv)))
        if r == 1:
            places(0, 2)
        for i, run in enumerate(MEET):
            a, b = run
            end = i == len(MEET) - 1
            if end:
                tt(f(N, 4 * a, 4 * b), f("at", 4 * a, 4 * b), f(X, 4 * a, 4 * b), add)
                if r == 1:
                    places(1, 2)
            else:
                for e in range(4):
                    meet(e, a, b)
            codes_x(r + 1, run)
            if not last:
                scores(r + 1, run, i)
                if not end:
                    for k in range(2):
                        keep_score("s", run, i, k)
                else:
                    if r == 1:
                        places(2, 2)
                    halve("v", r + 1, HALVES[1], C)
                    if r == 1:
                        places(3, 2)
                    keep_score("v", run, i, 0)
                    if r == 1:
                        places(4, 2)
            else:
                o, w = wide(run), kept(MEET, i)
                mm(bank(i, 0, o[1] - o[0]), f("vq"), f("vpl"), f("xq%d" % ROUNDS, o[0], o[1]), f("xp%d" % ROUNDS, o[0], o[1]))
                store("y", "oc%d" % i, T.oc[:, 4 * w[0]:4 * w[1]], T["xq%d" % ROUNDS][:, w[0]:w[1]].bitcast(dt.uint8), f("xq%d" % ROUNDS, w[0], w[1])[1])
                if end:
                    for k in range(4):
                        store("y", "os%d" % k, T.osc[4 * k:4 * k + 4, :], T["xp%d" % ROUNDS][32 * k:32 * k + 4, :], f("xp%d" % ROUNDS)[1])
                move("v" if end else "s", f("yt", a, b), bank(i, a - o[0], b - o[0]))
                store("s", "oy%d" % i, T.y[:, a:b], T.yt[:, a:b], f("yt", a, b)[1])
    for s in cnt:
        if seen["y"].get(s, 0) < cnt[s]:
            g.sync.wait_ge(T.sem[s], cnt[s])
